import numpy as np, ml_dtypes
CORES = [40,41,42,43,44,45,46,47]
N = 8
import mx_ref
BF = ml_dtypes.bfloat16
def gentries(a):
    return np.ascontiguousarray(a.reshape(8, 16, -1).transpose(0, 2, 1)).reshape(8, -1)
def gtable(e):
    e = np.asarray(e); return np.ascontiguousarray(e.reshape(8, -1, 16).transpose(0, 2, 1)).reshape(128, -1).astype(np.int32)
def gcols(t, e):
    v = np.concatenate([t.reshape(8, 16, -1, 4), np.zeros((8, 16, 1, 4), BF)], axis=2)
    return np.ascontiguousarray(np.stack([v[g][:, e[g]] for g in range(8)])).reshape(128, -1)
def tile(rs):
    return np.stack(rs, axis=2).reshape(128, -1).astype(BF)
def pick(q, e):
    c = np.concatenate([q[0].reshape(128, -1, 4), np.zeros((128, 1, 4), np.uint8)], axis=1); s = np.concatenate([q[1], np.ones((16, 1), np.uint8)], axis=1)
    return (np.ascontiguousarray(c[:, e].reshape(128, -1)), np.ascontiguousarray(s[:, e]))
def join(*qs):
    return (np.concatenate([q[0] for q in qs], axis=1), np.concatenate([q[1] for q in qs], axis=1))
def put(q, e, v):
    c, s = q[0].reshape(128, -1, 4).copy(), q[1].copy(); c[:, e] = v[0].reshape(128, -1, 4); s[:, e] = v[1]
    return (c.reshape(128, -1), s)
def pk(c, s):
    return (np.ascontiguousarray(c), mx_ref.live(s))
def emit(q):
    return q[0], q[1]
def packed(v, rng):
    q = [mx_ref.quantize(np.ascontiguousarray(v[r])) for r in range(N)]
    return np.stack([a for a, b in q]), np.stack([mx_ref.plane(b, rng) for a, b in q])
def values_of_codes():
    e, c = np.zeros((128, 128, 4), np.float32), np.zeros((128, 2, 4), np.uint8)
    e[np.arange(128), np.arange(128), 0] = 1
    c[:127, :, 0] = np.arange(256).reshape(2, 128).T[:127]
    return mx_ref.matmul(mx_ref.quantize(e.reshape(128, 512).astype(BF)), (c.reshape(128, 8), np.full((16, 2), 127, np.uint8))).T.reshape(-1).astype(np.float64)
CODE_VALUE, SCALE_VALUE = values_of_codes(), 2.0 ** (np.arange(256) - 127.0)
def decode(q):
    return (CODE_VALUE[q[0]].reshape(16, 8, -1, 4) * SCALE_VALUE[q[1]][:, None, :, None] + 0.0).reshape(128, -1).astype(np.float32)
def f(rng, *shape):
    return mx_ref.flush((rng.standard_normal(shape, dtype=np.float32) * np.exp2(rng.integers(-2, 3, shape[:-1] + (1,)))).astype(BF))
def wide(rng, *shape, cols=0):
    v = rng.standard_normal(shape, dtype=np.float32) * np.exp2(rng.integers(-12, 13, shape)).astype(np.float32)
    if cols: v *= np.repeat(np.exp2(rng.integers(-cols, cols + 1, shape[:-2] + (1, shape[-1] // 4))) * (rng.random(shape[:-2] + (1, shape[-1] // 4)) > 0.0625), 4, axis=-1).astype(np.float32)
    return mx_ref.flush(v.astype(BF))
C, STAGES = 320, 6
STEP = [1, 2, 4]
def numbers_of(rng):
    return {"x": np.array(f(rng, N, 128, 4 * C)), "u": np.array(f(rng, N, 128, 512)), "v": np.array(f(rng, N, 128, 512))}
def stored(a, b, s):
    return {"ta": np.stack([gtable(a[r]) for r in range(N)]), "tb": np.stack([gtable(b[r]) for r in range(N)]), "st": np.stack([gtable(s[r]) for r in range(N)])}
def lists(rng):
    e = np.tile(np.arange(C), (N, 8, 1))
    return stored(rng.permuted(e, axis=2), rng.permuted(e, axis=2), rng.permuted(e, axis=2))
def layers(rng):
    return np.array(f(rng, N, 128, 2048)).reshape(N, 8, 16, 4, 8, 16, 4)
def weights(rng, w):
    c, p = packed(np.ascontiguousarray(w).reshape(N, 128, 2048), rng)
    return {"wc": c, "ws": p}
def setup_inputs(rng):
    return {**numbers_of(rng), **lists(rng), **weights(rng, layers(rng))}
def setup_inputs_ties(rng):
    d = numbers_of(rng)
    o = rng.permutation(N)
    k = rng.integers(-1, 2, (2, N, 8, C)).astype(np.float32)
    k[0, o[1]] = 1
    x = d["x"].reshape(N, 8, 16, C, 4)
    x[:, :, [0, 1, 8]] = 0
    x[:, :, 0, :, 0] = k[0].astype(BF)
    x[:, :, 1, :, 0] = k[1].astype(BF)
    c = np.ones(N, np.float32)
    c[o[0]] = 0
    c[o[2]] = -1
    u = d["u"].reshape(N, 128, 128, 4)
    u[:, :, ::16] = 0
    for h in range(0, 128, 16):
        u[:, h, h, 0] = c.astype(BF)
        u[:, h + 8, h, 0] = c.astype(BF)
    w = layers(rng)
    w[:, :, :, :, :, [0, 1, 8]] = 0
    for g in range(8): w[:, g, 1, 0, g, 8, 0] = 32.0
    return {"x": x.reshape(N, 128, 4 * C), "u": u.reshape(N, 128, 512), "v": d["v"], **lists(rng), **weights(rng, w)}
def setup_inputs_near(rng):
    d = numbers_of(rng)
    o = rng.permutation(N) % 2
    k = np.where(o == 0, 2.0 ** -30, 1.0).astype(np.float32)
    x = np.zeros((N, 8, 16, C, 4), np.float32)
    s = rng.integers(-1, 2, (N, 8, C)) * k[:, None, None]
    x[:, :, 0, :, 0] = 1.125 * s
    x[:, :, 1, :, 0] = -1.25 * s
    for r in range(N):
        for g in rng.permutation(8)[:4]: x[r, g, 0, rng.integers(C), 0] = 2.0 ** 30 * rng.choice([-1.0, 1.0])
    x[:, :, 10, :, 0] = rng.integers(-1, 2, (N, 8, C)) * 2.0 ** -30
    x[:, :, 11, :, 0] = 2.0 ** -30
    u = d["u"].reshape(N, 128, 128, 4)
    u[:, :, ::16] = 0
    for h in range(0, 128, 16):
        u[:, h, h, 0] = (1.125 * k).astype(BF)
        u[:, h + 1, h, 0] = k.astype(BF)
        u[:, h + 8, h, 0] = k.astype(BF)
    w = np.zeros((N, 8, 16, 4, 8, 16, 4), np.float32)
    for g in range(8):
        w[:, g, 10, 0, g, 8, 0] = 2.0 ** -7
        w[:, g, 11, 0, g, 9, 0] = 2.0 ** 7
    for r in range(N):
        for g in rng.permutation(8)[:4]:
            w[r, g, 10, 0, g, 8, 0] = 2.0 ** -11
            w[r, g, 10, 0, g, 13, 0] = -2.0 ** -11
            w[r, g, 12, 0, g, 8, 0] = 2.0 ** -8
            w[r, g, 12, 0, g, 13, 0] = 2.0 ** -8
            w[r, g, 11, 0, g, 9, 0] = 2.0 ** 5
            u[r, 16 * g + 8, 16 * g, 0] = 1.125 * float(k[r])
            u[r, 16 * g + 13, 16 * g, 0] = float(k[r])
    return {"x": x.reshape(N, 128, 4 * C).astype(BF), "u": u.reshape(N, 128, 512), "v": d["v"], **lists(rng), **weights(rng, w.astype(BF))}
def setup_inputs_odd(rng):
    d = numbers_of(rng)
    x = (1.0 + (2 * rng.integers(0, 64, (N, 8, 16, C, 4)) + 1) * 2.0 ** -7) * np.exp2(-rng.integers(0, 7, (N, 8, 16, C, 4)).astype(np.float64)) * rng.choice([-1.0, 1.0], (N, 8, 16, C, 4))
    x[:, :, 0, :, 0] = 1.96875 * 2.0 ** 8 * rng.choice([-1.0, 1.0], (N, 8, C))
    x[:, :, 1:3] = 0
    x[:, :, 1, :, 0] = (8 + rng.integers(0, 2, (N, 8, C))) * 2.0 ** -8
    x[:, :, 2, :, 0] = -2.0 ** -5
    a = np.exp2(rng.integers(-3, 4, (N, 8, C)).astype(np.float64))
    x[:, :, 8:] = 0
    x[:, :, 8, :, 0] = 1.125 * a
    x[:, :, 11, :, 0] = (8 + rng.integers(0, 2, (N, 8, C))) * 2.0 ** -7 * a
    x[:, :, 12, :, 0] = 2.0 ** -4 * a
    u = d["u"].reshape(N, 128, 128, 4)
    u[:, :, ::16] = 0
    for h in range(0, 128, 16):
        for i in (1, 2, 9, 10): u[:, h + i, h, 0] = 1.0
    w = layers(rng)
    w[:, :, :3] = 0
    w[:, :, :, :, :, :3] = 0
    w[:, :, :, :, :, 8:] = 0
    for g in range(8):
        w[:, g, 8, 0, g, 8, 0] = 28.0
        w[:, g, 11, 0, g, 9, 0] = 2.0 ** -5
        w[:, g, 12, 0, g, 10, 0] = -2.0 ** -5
    return {"x": x.astype(np.float32).reshape(N, 128, 4 * C).astype(BF), "u": u.reshape(N, 128, 512), "v": d["v"], **lists(rng), **weights(rng, w)}
def setup_inputs_ends(rng):
    d = numbers_of(rng)
    o, e, h = rng.permutation(N) % 4, rng.permutation(N) % 4, rng.permutation(N) % 2
    s = rng.choice([-1.0, 1.0], (N, 8, 8, C, 4))
    s[o == 0] = -1
    s[o == 1] = rng.choice([-1.0, 1.0], (N, 1, 1, C, 1))[o == 1]
    low = s * (0.9 + 0.1 * rng.random((N, 8, 8, C, 4))) * 2.0 ** 30
    low[o == 3] = s[o == 3] * 2.0 ** -30
    x = d["x"].astype(np.float32).reshape(N, 8, 16, C, 4)
    x[:, :, :8] = low
    size = np.where(o == 3, 2.0 ** -30, 2.0 ** 30)
    c = np.stack([rng.permutation(8) % 2 * 2.0 - 1.0 for r in range(N)]) * size[:, None]
    u = d["u"].reshape(N, 128, 128, 4)
    u[:, :, ::16] = c.astype(np.float32).astype(BF)[:, None, :, None]
    v = rng.choice([-1.0, 1.0], (N, 128, 512)) * size[:, None, None]
    a, b, t = [rng.integers(0, C, (N, 8, C)) for i in range(3)]
    a[e == 0], b[e == 0], t[e == 0] = C - 1, C - 1, C - 1
    a[e == 1], b[e == 1], t[e == 1] = 0, C - 1, 0
    a[e == 2], b[e == 2], t[e == 2] = C - 1 - np.arange(C), np.arange(C), (np.arange(C) + 1) % 2 * (C - 1)
    w = np.zeros((N, 128, 4, 128, 4), np.float32)
    i = np.flatnonzero(np.arange(128) % 16 >= 8)
    for k in range(4): w[:, i, k, i, k] = np.where(h == 0, 2.0 ** 8, 2.0 ** -8)[:, None] * rng.choice([-1.0, 1.0], (N, 64))
    return {"x": x.reshape(N, 128, 4 * C).astype(BF), "u": u.reshape(N, 128, 512), "v": v.astype(np.float32).astype(BF), **stored(a, b, t), **weights(rng, w.astype(BF))}
def setup_inputs_spread(rng):
    d = setup_inputs(rng)
    d["x"] = wide(rng, N, 128, 4 * C, cols=6)
    return d
def check_inputs(d):
    b = []
    for k in ("x", "u", "v"):
        a = np.abs(d[k].astype(np.float32))
        if not (np.isfinite(a).all() and ((a == 0) | (a >= 2.0 ** -30) & (a <= 2.0 ** 30)).all()): b.append("a value of " + k)
    for k in ("ta", "tb", "st"):
        if not ((d[k] >= 0) & (d[k] < C)).all(): b.append("an entry of " + k)
    none, least, most = [emit(mx_ref.quantize(np.full((128, 16), k, np.float32).astype(BF)))[1][0, 0] for k in (0.0, 2.0 ** -8, 2.0 ** 8)]
    for r in range(N):
        if ((d["wc"][r] == 0x7F) | (d["wc"][r] == 0xFF)).any(): b.append("wc: a code that is no number")
        s = mx_ref.live(d["ws"][r])
        if ((s != none) & ((s < least) | (s > most))).any(): b.append("ws: a scale out of range")
    return b
def at(t, s):
    return np.take_along_axis(t, s, axis=2)
def reference(x, u, v, ta, tb, st, wc, ws):
    qu = [mx_ref.quantize(u[r]) for r in range(N)]
    lay = [pk(wc[r], ws[r]) for r in range(N)]
    a, b, s = [np.stack([gentries(k[r]) for r in range(N)]).astype(np.int64) for k in (ta, tb, st)]
    now = [x[r] for r in range(N)]
    for step in STEP:
        q = [mx_ref.quantize(now[r]) for r in range(N)]
        bit = np.stack([mx_ref.matmul(qu[r], q[r])[::16] > 0 for r in range(N)])
        for k in range(STAGES):
            right = np.roll(at(bit, s), -1, axis=2)
            s = np.where(right, at(b, s), at(a, s))
        z = [gcols(decode(q[r]).astype(BF), s[r]) for r in range(N)]
        qz = [mx_ref.quantize(z[r]) for r in range(N)]
        made, change = [], []
        for r in range(N):
            p = r ^ step
            h = tile([mx_ref.matmul(pick(lay[r], np.arange(128 * k, 128 * k + 128)), qz[p]) * np.float32(0.03125) for k in range(4)])
            change.append(mx_ref.matmul(qu[r], mx_ref.quantize(h))[::16] > 0)
            made.append((z[r].astype(np.float32) + gcols(h, s[p]).astype(np.float32)).astype(BF))
        c = np.stack(change)
        a, b = np.where(c, b, a), np.where(c, a, b)
        now = made
    y, op = np.zeros((N, 128, C), np.float32), np.zeros((N, 8, 3 * C), np.float32)
    oc, osc = np.zeros((N, 128, 4 * C), np.uint8), np.zeros((N, 16, C), np.uint8)
    for r in range(N):
        q = mx_ref.quantize(now[r])
        y[r] = mx_ref.matmul(mx_ref.quantize(v[r]), q)
        op[r] = np.concatenate([s[r], a[r], b[r]], axis=1)
        oc[r], osc[r] = emit(q)
    return {"y": y, "op": op, "oc": oc, "osc": osc}

@@ -1,0 +1,350 @@
+from concourse.mybir import dt, AluOpType, ActivationFunctionType
+
+STEP = [1, 2, 4]
+C, STAGES = 320, 6
+L = 2048
+BIG = 4096
+UP = 2.0 ** 60
+CUT = 10
+SCRATCH = {}
+
+
+def _declare(names, where, cols, dtype):
+    for n in names.split():
+        SCRATCH[n] = (where, [128, cols], dtype)
+
+
+F8, U8 = "float8_e4m3fn_x4", "uint8"
+_declare("sti tai tbi kp kk k20 e16 ee qq ic cc", "sbuf", 20, "int32")
+_declare("d32 dd", "sbuf", 32, "int32")
+_declare("lui", "sbuf", 8, "int32")
+_declare("lu", "sbuf", 8, "uint16")
+_declare("lk rho la lb ls lfa lfb sn0 sn1 sn2 pl0 pl1 pl2", "sbuf", 20, "uint16")
+_declare("lc o0 o1 sc", "sbuf", 22, "uint16")
+_declare("rr", "sbuf", 60, "float32")
+_declare("pp", "sbuf", 160, "float32")
+_declare("sm", "sbuf", 8, "float32")
+_declare("M G0 G1 E0 E1", "sbuf", 336, "float32")
+_declare("M0 idn b0 b4 uu b4s g1 g2 g3 x12 x320 fin tt pk NR EN yb", "sbuf", C, "float32")
+_declare("W W6", "sbuf", 3016, "float32")
+_declare("W4", "sbuf", 1280, "float32")
+_declare("ob", "sbuf", 960, "float32")
+_declare("one dg", "sbuf", 128, "bfloat16")
+_declare("ui vi", "sbuf", 512, "bfloat16")
+_declare("et", "sbuf", 2048, "bfloat16")
+_declare("xi ht z za xn0 xn1 xn2", "sbuf", 4 * C, "bfloat16")
+_declare("t0 t1 t2 t3 w0 w1 w2 w3 h0 h1 h2 h3", "sbuf", C, "bfloat16")
+for _q, _p, _n in (("wq", "wp", 512), ("uq", "us", 128), ("urq", "urs", 128), ("vq", "vs", 128), ("eq", "es", 512), ("hq", "hp", C), ("zq", "zp", C)):
+    _declare(_q, "sbuf", _n, F8)
+    _declare(_p, "sbuf", _n, U8)
+_declare("rq0 rq1 rq2 xq0 xq1 xq2 xq3", "sbuf", C, F8)
+_declare("rp0 rp1 rp2 xs0 xs1 xs2 xs3", "sbuf", C, U8)
+_declare("ps0 ps1 ps2 ps3 ps4 ps5 ps6", "psum", 512, "float32")
+SEMAPHORES = ("cv ct ca cg sent gotl0 gotl1 gotl2 gotz0 gotz1 gotz2 ld_st ld_x ld_ta ld_tb ld_u ld_wc ld_ws ld_v "
+              "sv_y sv_ops sv_opt sv_oc sv_os0 sv_os1 sv_os2 sv_os3").split()
+
+
+def rank_program(g, core, T, topo):
+    rank = T.rank_of(core)
+    if rank is None:
+        return
+    A, ACT = AluOpType, ActivationFunctionType
+    queues = {"v": g.vector, "t": g.tensor, "a": g.scalar, "g": g, "y": g.sync}
+    counter = {"v": "cv", "t": "ct", "a": "ca", "g": "cg"}
+    count = {}
+    known = {q: {} for q in queues}
+    told = {}
+    wrote, read = {}, {}
+
+    def learn(q, tokens):
+        need = {}
+        for s, n in tokens:
+            need[s] = max(need.get(s, 0), n)
+        for s in sorted(need):
+            n = need[s]
+            if known[q].get(s, 0) >= n:
+                continue
+            queues[q].wait_ge(T.sem[s], n)
+            known[q][s] = n
+            for k, m in told.get((s, n), {}).items():
+                known[q][k] = max(known[q].get(k, 0), m)
+
+    def op(q, call, rd, wr, sem=None, inc=1):
+        need = []
+        for k in rd:
+            need += wrote.get(k, [])
+        for k in wr:
+            need += wrote.get(k, []) + read.get(k, [])
+        learn(q, need)
+        s = sem or counter[q]
+        call().then_inc(T.sem[s], inc)
+        count[s] = count.get(s, 0) + inc
+        tok = (s, count[s])
+        told[tok] = dict(known[q])
+        for k in rd:
+            read.setdefault(k, []).append(tok)
+        for k in wr:
+            wrote[k], read[k] = [tok], []
+
+    V, S, P = g.vector, g.scalar, g.tensor
+
+    def load(q, name, out, in_, key):
+        op(q, lambda: queues[q].dma_start(out, in_), [], [key], sem="ld_" + name, inc=16)
+
+    def store(name, out, in_, rd):
+        op("y", lambda: g.sync.dma_start(out, in_), rd, [], sem="sv_" + name, inc=16)
+
+    def iota(out, pattern, base, cm, wr, f32=False):
+        if f32:
+            op("g", lambda: g.iota(out, pattern, base, cm, allow_small_or_imprecise_dtypes=True), [], [wr])
+        else:
+            op("g", lambda: g.iota(out, pattern, base, cm), [], [wr])
+
+    def cpg(out, in_, rd, wr):
+        op("g", lambda: g.affine_select(out, in_, [[1, C]], A.is_ge, 0.0, 0, 0), rd, wr)
+
+    def ts(out, in0, s1, s2, o0, o1, rd, wr):
+        if o1 is None:
+            op("v", lambda: V.tensor_scalar(out, in0, s1, None, o0), rd, wr)
+        else:
+            op("v", lambda: V.tensor_scalar(out, in0, s1, s2, o0, o1), rd, wr)
+
+    def tt(out, a, b, o, rd, wr):
+        op("v", lambda: V.tensor_tensor(out, a, b, o), rd, wr)
+
+    def cpv(out, in_, rd, wr):
+        op("v", lambda: V.tensor_copy(out, in_), rd, wr)
+
+    def cpa(out, in_, rd, wr):
+        op("a", lambda: S.activation(out, in_, ACT.Copy), rd, wr)
+
+    def scan(out, d0, d1, init, o0, o1, rd, wr):
+        op("v", lambda: V.tensor_tensor_scan(out, d0, d1, init, o0, o1), rd, wr)
+
+    def plus(out, a, b, rd, wr):
+        scan(out, a, b, float(BIG), A.min, A.add, rd, wr)
+
+    def quant(codes, plane, tile, rd, wr):
+        op("v", lambda: V.quantize_mx(codes, plane, tile), rd, wr)
+
+    def mm(bank, lq, lp, rq, rp, rd):
+        op("t", lambda: P.matmul_mx(T["ps%d" % bank][:, 0:C], lq, lp, rq, rp, True, True), rd, ["ps%d" % bank])
+
+    load("y", "st", T.sti[:], T.st[:], "sti")
+    load("y", "x", T.xi[:], T.x[:], "xi")
+    load("a", "u", T.ui[:], T.u[:], "ui")
+    load("a", "ta", T.tai[:], T.ta[:], "tai")
+    load("y", "tb", T.tbi[:], T.tb[:], "tbi")
+    learn("y", wrote["xi"])
+    load("y", "wc", T.wq[:, :].bitcast(dt.uint8), T.wc[:, :], "wq")
+    load("y", "ws", T.wp[:, :], T.ws[:, :], "wp")
+    load("y", "v", T.vi[:], T.v[:], "vi")
+
+    op("v", lambda: V.memset(T.one[:], 1.0), [], ["one"])
+    iota(T.kp[:], [[0, 20]], 0, 1, "kp")
+    iota(T.d32[:], [[1, 2], [1, 16]], 127, -1, "d32")
+    iota(T.lui[:], [[16, 8]], 0, 0, "lui")
+    op("g", lambda: g.affine_select(T.dg[:], T.one[:], [[-1, 128]], A.is_equal, 0.0, 0, 1), ["one"], ["dg"])
+    iota(T.ic[:], [[-1, 20]], 19, 0, "ic")
+    iota(T.e16[:], [[16, 20]], 0, 0, "e16")
+    iota(T.idn[:], [[1, C]], 1, 0, "idn", True)
+    iota(T.b0[:], [[3, C]], 3 + BIG, 0, "b0", True)
+
+    def unnamed(w):
+        iota(T[w][:, 0:3], [[0, 3]], BIG + 3, 0, w + "x", True)
+        iota(T[w][:, 963:2051], [[0, 1088]], BIG + 3, 0, w + "y", True)
+
+    unnamed("W")
+    op("v", lambda: V.memset(T.et[:, 0:1024], 0.0), [], ["etz"])
+    cpa(T.et[:, 1024:2048], T.et[:, 0:1024], ["etz"], ["ety"])
+    ts(T.kk[:], T.kp[:], 15, None, A.bitwise_and, None, ["kp"], ["kk"])
+    ts(T.dd[:], T.d32[:], 15, None, A.bitwise_and, None, ["d32"], ["dd"])
+    cpv(T.lk[:], T.kk[:], ["kk"], ["lk"])
+    cpv(T.lu[:], T.lui[:], ["lui"], ["lu"])
+    ts(T.pp[:, 0:32], T.dd[:], 0, 1.0 / UP / L, A.is_equal, A.mult, ["dd"], ["p0"])
+    ts(T.pp[:, 32:64], T.dd[:], 1, UP, A.is_equal, A.mult, ["dd"], ["p1"])
+    ts(T.pp[:, 64:96], T.dd[:], 2, None, A.is_ge, None, ["dd"], ["p2"])
+    ts(T.sm[:, 2:3], T.dd[:, 16:17], 2, UP, A.is_equal, A.mult, ["dd"], ["m1"])
+    ts(T.sm[:, 3:4], T.dd[:, 16:17], 1, None, A.is_ge, None, ["dd"], ["m2"])
+    ts(T.sm[:, 0:1], T.kk[:, 0:1], 15, None, A.is_equal, None, ["kk"], ["c1"])
+    ts(T.sm[:, 1:2], T.kk[:, 0:1], 15, 1.0 / UP, A.is_lt, A.mult, ["kk"], ["c2"])
+    ts(T.k20[:], T.kk[:], 20, None, A.mult, None, ["kk"], ["k20"])
+    tt(T.pp[:, 96:128], T.pp[:, 32:64], T.pp[:, 64:96], A.add, ["p1", "p2"], ["p12"])
+    tt(T.sm[:, 4:5], T.sm[:, 2:3], T.sm[:, 3:4], A.max, ["m1", "m2"], ["m3"])
+    tt(T.sm[:, 5:6], T.sm[:, 0:1], T.sm[:, 1:2], A.add, ["c1", "c2"], ["cp"])
+    tt(T.pp[:, 128:160], T.pp[:, 96:128], T.pp[:, 0:32], A.add, ["p12", "p0"], ["pm"])
+    tt(T.cc[:], T.k20[:], T.ic[:], A.add, ["k20", "ic"], ["cc"])
+    tt(T.ee[:], T.e16[:], T.kk[:], A.add, ["e16", "kk"], ["ee"])
+    cpv(T.M[:, 0:16], T.pp[:, 128:144], ["pm"], ["Ma"])
+    cpv(T.lc[:, 1:21], T.cc[:], ["cc"], ["lc1"])
+    cpv(T.lc[:, 0:1], T.k20[:, 0:1], ["k20"], ["lc0"])
+    ts(T.qq[:], T.ee[:], -9.5, 0.05, A.add, A.mult, ["ee"], ["qq"])
+    ts(T.rr[:, 0:20], T.ee[:], -16.0, 304.0, A.mult, A.add, ["ee"], ["r1"])
+    ts(T.rr[:, 20:40], T.qq[:], 321.0, None, A.mult, None, ["qq"], ["r2"])
+    tt(T.rr[:, 40:60], T.rr[:, 0:20], T.rr[:, 20:40], A.add, ["r1", "r2"], ["r3"])
+    cpv(T.rho[:], T.rr[:, 40:60], ["r3"], ["rho"])
+    CP = T.sm[:, 5:6]
+    for b in range(4):
+        cpa(T.et[:, 512 * b + b:512 * b + 512:4], T.dg[:], ["dg", "etz", "ety"], ["et%d" % b])
+    cpa(T.M[:, 16:336], T.pp[:, 144:160].indirect(T.lk[:]), ["pm", "lk"], ["Mb"])
+    cpv(T.ls[:], T.sti[:], ["sti"], ["ls"])
+    cpa(T.NR[:], T.idn[:].indirect(T.ls[:]), ["idn", "ls"], ["NRa", "NRb"])
+    cpa(T.G1[:, :], T.NR[:].indirect(T.lc[:, 0:21]), ["NRa", "NRb", "lc0", "lc1"], ["G1a", "G1b"])
+    quant(T.eq[:], T.es[:], T.et[:], ["et0", "et1", "et2", "et3", "etz", "ety"], ["eq"])
+    tt(T.M[:, 16:17], T.sm[:, 4:5], T.pp[:, 16:17], A.max, ["m3", "p0"], ["Mb"])
+
+    quant(T.uq[:], T.us[:], T.ui[:], ["ui"], ["uq"])
+    cpv(T.urq[:, 0:128].bitcast(dt.uint32), T.uq[:, 0:128].bitcast(dt.uint32).indirect(T.lu[:, 0:8]), ["uq", "lu"], ["urq"])
+    cpa(T.urs[:, 0:128], T.us[:, 0:128].indirect(T.lu[:, 0:8]), ["uq", "lu"], ["urs"])
+    cpv(T.la[:], T.tai[:], ["tai"], ["la"])
+    cpv(T.lb[:], T.tbi[:], ["tbi"], ["lb"])
+
+    def scores(r):
+        mm(4, T.urq[:], T.urs[:], T["xq%d" % r][:], T["xs%d" % r][:], ["urq", "urs", "xq%d" % r])
+
+    def unpack(b, q, p):
+        mm(b, T.eq[:, 128 * b:128 * b + 128], T.es[:, 128 * b:128 * b + 128], T[q][:], T[p][:], ["eq", q])
+
+    def row(G, E):
+        scan(T[E][:, :], T.M[:, :], T[G][:, :], 0.0, A.mult, A.add, [G + "a", G + "b", "Ma", "Mb"], [E])
+
+    def offsets(E, o, less):
+        ts(T[o][:, 1:21], T[E][:, 31:336:16], CP, -float(less), A.mult, A.add, [E, "cp"], [o + "m"])
+        ts(T[o][:, 0:1], T[E][:, 335:336], CP, -float(less), A.mult, A.add, [E, "cp"], [o + "d"])
+
+    def partner(r):
+        other = T.cores[rank ^ STEP[r]]
+        return topo.addr(other)[0:2] + (topo.mask(core, other), len(topo.engines(core, other)))
+
+    def send_state(r):
+        rid, pid, mask, ne = partner(r)
+        xq, xs, rq, rp, sem = [n + str(r) for n in ("xq", "xs", "rq", "rp", "gotz")]
+        learn("g", wrote[xq])
+        g.remote_dma(T[rq][:, :].bitcast(dt.uint8), T[xq][:, :].bitcast(dt.uint8), T.sem[sem], T.sem.sent, pid, rid, mask)
+        g.remote_dma(T[rp][:, :], T[xs][:, :], T.sem[sem], T.sem.sent, pid, rid, mask)
+        count["sent"] = count.get("sent", 0) + 2 * ne
+        wrote[rq] = [(sem, 2 * ne)]
+
+    quant(T.xq0[:], T.xs0[:], T.xi[:], ["xi"], ["xq0"])
+    scores(0)
+    for b in range(4):
+        unpack(b, "xq0", "xs0")
+    row("G1", "E1")
+    offsets("E1", "sc", 1)
+    send_state(0)
+    cpa(T.W6[:, 3:961:3], T.idn[:].indirect(T.la[:]), ["idn", "la"], ["W60"])
+    cpa(T.W6[:, 4:962:3], T.idn[:].indirect(T.lb[:]), ["idn", "lb"], ["W61"])
+    W6K = ["W60", "W61", "W62", "W6x", "W6y", "W63", "W64", "W65"]
+    WK = ["W0", "W1", "W2", "W3", "W4a1", "W4b1", "W5", "Wx", "Wy"]
+    less = BIG + BIG // L
+    ts(T.tt[:], T.ps4[:, 0:C], 0.0, float(L), A.is_gt, A.mult, ["ps4"], ["tt"])
+    plus(T.pk[:], T.tt[:], T.b0[:], ["tt", "b0"], ["pk"])
+
+    for r in range(3):
+        rid, pid, mask, ne = partner(r)
+        rq, rp, sn, pl, xn = [n + str(r) for n in ("rq", "rp", "sn", "pl", "xn")]
+        cpa(T.W[:, 3:961:3], T.pk[:].indirect(T.la[:]), ["pk", "la"], ["W0"])
+        cpv(T.G0[:, :], T.pk[:].indirect(T.sc[:, 0:21]), ["pk", "scm", "scd"], ["G0a", "G0b"])
+        cpv(T.W[:, 4:962:3], T.pk[:].indirect(T.lb[:]), ["pk", "lb"], ["W1"])
+        cpa(T.W[:, 5:963:3], T.W[:, 3:961:3], ["W0"], ["W2"])
+        cpg(T.W[:, 2051:3009:3], T.W[:, 3:961:3], ["W0"], ["W3"])
+        cpa(T.W[:, 2053:3011:3], T.W[:, 3:961:3], ["W0"], ["W5"])
+        row("G0", "E0")
+        cpv(T.W[:, 2052:2530:3], T.W[:, 4:482:3], ["W1"], ["W4a1"])
+        cpa(T.W[:, 2532:3010:3], T.W[:, 484:962:3], ["W1"], ["W4b1"])
+        offsets("E0", "o0", less)
+        if r == 0:
+            unnamed("W6")
+            cpg(T.W6[:, 5:963:3], T.W6[:, 3:961:3], ["W60"], ["W62"])
+            cpg(T.W6[:, 2051:3009:3], T.W6[:, 3:961:3], ["W60"], ["W63"])
+            cpg(T.W6[:, 2052:3010:3], T.W6[:, 4:962:3], ["W61"], ["W64"])
+            cpg(T.W6[:, 2053:3011:3], T.W6[:, 3:961:3], ["W60"], ["W65"])
+            iota(T.b4[:], [[1, C]], BIG, 0, "b4", True)
+        gaps = [(T["t%d" % b][:], T["ps%d" % b][:, 0:C], ["ps%d" % b], ["t%d" % b], b) for b in range(4)]
+        gaps += [(T["w%d" % b][:], T["ps%d" % b][:, 0:C], ["ps%d" % b], ["w%d" % b], None) for b in range(2)]
+        for n in range(1, STAGES + 1):
+            o, G, E, on = "o%d" % ((n + 1) % 2), "G%d" % (n % 2), "E%d" % (n % 2), "o%d" % (n % 2)
+            win, wk = (T.W, WK) if n < STAGES else (T.W6, W6K)
+            cpv(T[G][:, 0:16 * CUT], win[:, 0:3011].indirect(T[o][:, 0:CUT]), wk + [o + "m", o + "d"], [G + "a"])
+            cpa(T[G][:, 16 * CUT:336], win[:, 0:3011].indirect(T[o][:, CUT:21]), wk + [o + "m"], [G + "b"])
+            if n < STAGES:
+                for out, in_, rd, wr, b in [gaps.pop(0) for i in range(2 if n == 1 else 1)]:
+                    cpa(out, in_, rd, wr)
+                    if b is not None:
+                        unpack(b, rq, rp)
+                row(G, E)
+                offsets(E, on, less)
+        cpv(T.NR[:, 0:160], T.G0[:, 16:336].indirect(T.rho[:, 0:10]), ["G0a", "G0b", "rho"], ["NRa"])
+        cpa(T.NR[:, 160:320], T.G0[:, 16:336].indirect(T.rho[:, 10:20]), ["G0a", "G0b", "rho"], ["NRb"])
+        if r == 0:
+            cpa(T.M0[:], T.pp[:, 112:128].indirect(T.lk[:]), ["p12", "lk"], ["M0"])
+        scan(T.EN[:], T.M[:, 16:336], T.NR[:], 0.0, A.mult, A.add, ["NRa", "NRb", "Mb"], ["EN"])
+        ts(T[sn][:], T.EN[:, 15:320:16], CP, -1.0, A.mult, A.add, ["EN", "cp"], [sn])
+        learn("g", wrote[sn])
+        g.remote_dma(T[pl][:, :], T[sn][:, :], T.sem["gotl%d" % r], T.sem.sent, pid, rid, mask)
+        count["sent"] += ne
+        wrote[pl] = [("gotl%d" % r, ne)]
+        for b in range(4):
+            (cpv if b < 2 else cpa)(T.z[:, b:4 * C:4], T["t%d" % b][:].indirect(T[sn][:]), ["t%d" % b, sn], ["z%d" % b])
+        for b in range(2, 4):
+            (cpv if b == 2 else cpa)(T["w%d" % b][:], T["ps%d" % b][:, 0:C], ["ps%d" % b], ["w%d" % b])
+        for b in range(4):
+            (cpv if b < 2 else cpa)(T.za[:, b:4 * C:4], T["w%d" % b][:].indirect(T[pl][:]), ["w%d" % b, pl], ["za%d" % b])
+        quant(T.zq[:], T.zp[:], T.za[:], ["za%d" % b for b in range(4)], ["zq"])
+        for b in range(4):
+            mm(b, T.wq[:, 128 * b:128 * b + 128], T.wp[:, 128 * b:128 * b + 128], T.zq[:], T.zp[:], ["wq", "wp", "zq"])
+        if r < 2:
+            row("G0", "E1")
+            offsets("E1", "sc", 1)
+        if r == 0:
+            quant(T.vq[:], T.vs[:], T.vi[:], ["vi"], ["vq"])
+        if r == 2:
+            ts(T.x320[:], T.x12[:], 320.0, None, A.mult, None, ["x12"], ["x320"])
+            plus(T.b4s[:], T.x320[:], T.b4[:], ["x320", "b4"], ["b4s"])
+            op("a", lambda: S.activation(T.ob[:, 0:320], T.NR[:], ACT.Identity, bias=-1.0), ["NRa", "NRb"], ["obs"])
+            store("ops", T.op[:, 0:320], T.ob[0:128:16, 0:320], ["obs"])
+        for b in range(4):
+            hb, pb = T["h%d" % b], T["ps%d" % b]
+            op("a", lambda: S.activation(hb[:], pb[:, 0:C], ACT.Copy, scale=0.03125), ["ps%d" % b], ["h%d" % b])
+            tt(T[xn][:, b:4 * C:4], hb[:].indirect(T[pl][:]), T.z[:, b:4 * C:4], A.add, ["h%d" % b, pl, "z%d" % b], [xn + str(b)])
+        for b in range(4):
+            cpa(T.ht[:, b:4 * C:4], T["h%d" % b][:], ["h%d" % b], ["ht%d" % b])
+        if r == 1:
+            for i, key in enumerate(("W4a", "W4b", "W4c", "W4d")):
+                cpg(T.W4[:, 320 * i:320 * i + 320], T.W6[:, 3 + i % 2:961 + i % 2:3], ["W6%d" % (i % 2)], [key])
+        xq, xs = "xq%d" % (r + 1), "xs%d" % (r + 1)
+        if r < 2:
+            quant(T[xq][:], T[xs][:], T[xn][:], [xn + str(b) for b in range(4)], [xq])
+            scores(r + 1)
+            send_state(r + 1)
+            quant(T.hq[:], T.hp[:], T.ht[:], ["ht%d" % b for b in range(4)], ["hq"])
+            mm(5, T.urq[:], T.urs[:], T.hq[:], T.hp[:], ["urq", "urs", "hq"])
+            for b in range(4):
+                unpack(b, xq, xs)
+            gk = "g%d" % (r + 1)
+            ts(T.tt[:], T.ps4[:, 0:C], 0.0, float(L), A.is_gt, A.mult, ["ps4"], ["tt"])
+            ts(T[gk][:], T.ps5[:, 0:C], 0.0, None, A.is_gt, None, ["ps5"], [gk])
+            plus(T.uu[:], T.tt[:], T.b0[:], ["tt", "b0"], ["uu"])
+            if r == 1:
+                tt(T.x12[:], T.g1[:], T.g2[:], A.not_equal, ["g1", "g2"], ["x12"])
+                gk = "x12"
+            plus(T.pk[:], T[gk][:], T.uu[:], [gk, "uu"], ["pk"])
+    quant(T.hq[:], T.hp[:], T.ht[:], ["ht%d" % b for b in range(4)], ["hq"])
+    mm(5, T.urq[:], T.urs[:], T.hq[:], T.hp[:], ["urq", "urs", "hq"])
+    quant(T.xq3[:], T.xs3[:], T.xn2[:], ["xn2%d" % b for b in range(4)], ["xq3"])
+    mm(6, T.vq[:], T.vs[:], T.xq3[:], T.xs3[:], ["vq", "xq3"])
+    store("oc", T.oc[:, :], T.xq3[:, :].bitcast(dt.uint8), ["xq3"])
+    for k in range(4):
+        store("os%d" % k, T.osc[4 * k:4 * k + 4, :], T.xs3[32 * k:32 * k + 4, :], ["xq3"])
+    cpa(T.yb[:], T.ps6[:, 0:C], ["ps6"], ["yb"])
+    store("y", T.y[:, :], T.yb[:], ["yb"])
+    ts(T.g3[:], T.ps5[:, 0:C], 0.0, 320.0, A.is_gt, A.mult, ["ps5"], ["g3"])
+    plus(T.fin[:], T.g3[:], T.b4s[:], ["g3", "b4s"], ["fin"])
+    scan(T.EN[:], T.M0[:], T.fin[:], 0.0, A.mult, A.add, ["fin", "M0"], ["EN"])
+    ts(T.lfa[:], T.EN[:, 15:320:16], CP, -float(BIG), A.mult, A.add, ["EN", "cp"], ["lfa"])
+    ts(T.lfb[:], T.EN[:, 15:320:16], CP, 320.0 - BIG, A.mult, A.add, ["EN", "cp"], ["lfb"])
+    w4 = ["W4a", "W4b", "W4c", "W4d"]
+    op("a", lambda: S.activation(T.ob[:, 320:640], T.W4[:, :].indirect(T.lfa[:]), ACT.Identity, bias=-1.0), w4 + ["lfa"], ["oba"])
+    ts(T.ob[:, 640:960], T.W4[:, :].indirect(T.lfb[:]), -1.0, None, A.add, None, w4 + ["lfb"], ["obb"])
+    store("opt", T.op[:, 320:960], T.ob[0:128:16, 320:960], ["oba", "obb"])
+    learn("g", [(s, n) for s, n in count.items()])

@@ -2,9 +2,11 @@ from concourse.mybir import dt, AluOpType, ActivationFunctionType
 
 STEP = [1, 2, 4]
 C, STAGES = 320, 6
-L = 2048
+L = 1536
 BIG = 4096
-UP = 2.0 ** 60
+UP = 2.0 ** 24
+MID = 482
+WIN = L + 963
 CUT = 10
 SCRATCH = {}
 
@@ -24,9 +26,12 @@ _declare("lc o0 o1 sc", "sbuf", 22, "uint16")
 _declare("rr", "sbuf", 60, "float32")
 _declare("pp", "sbuf", 160, "float32")
 _declare("sm", "sbuf", 8, "float32")
-_declare("M G0 G1 E0 E1", "sbuf", 336, "float32")
-_declare("M0 idn b0 b4 uu b4s g1 g2 g3 x12 x320 fin tt pk NR EN yb", "sbuf", C, "float32")
-_declare("W W6", "sbuf", 3016, "float32")
+_declare("G6", "sbuf", 336, "float32")
+_declare("M", "sbuf", 336, "bfloat16")
+_declare("G0 G1 E0 E1", "sbuf", 336, "float16")
+_declare("NR EN", "sbuf", C, "float16")
+_declare("M0 idn b0 b4 uu b4s g1 g2 g3 x12 x320 fin tt pk yb", "sbuf", C, "float32")
+_declare("W W6", "sbuf", WIN + 5, "float32")
 _declare("W4", "sbuf", 1280, "float32")
 _declare("ob", "sbuf", 960, "float32")
 _declare("one dg", "sbuf", 128, "bfloat16")
@@ -118,6 +123,12 @@ def rank_program(g, core, T, topo):
     def cpa(out, in_, rd, wr):
         op("a", lambda: S.activation(out, in_, ACT.Copy), rd, wr)
 
+    def small(q, out, in_, less, rd, wr):
+        if q == "a":
+            op("a", lambda: S.activation(out, in_, ACT.Identity, bias=-less / UP, scale=1.0 / UP), rd, wr)
+        else:
+            ts(out, in_, -float(less), 1.0 / UP, A.add, A.mult, rd, wr)
+
     def scan(out, d0, d1, init, o0, o1, rd, wr):
         op("v", lambda: V.tensor_tensor_scan(out, d0, d1, init, o0, o1), rd, wr)
 
@@ -151,8 +162,8 @@ def rank_program(g, core, T, topo):
     iota(T.b0[:], [[3, C]], 3 + BIG, 0, "b0", True)
 
     def unnamed(w):
-        iota(T[w][:, 0:3], [[0, 3]], BIG + 3, 0, w + "x", True)
-        iota(T[w][:, 963:2051], [[0, 1088]], BIG + 3, 0, w + "y", True)
+        iota(T[w][:, 0:3], [[0, 3]], 0, 0, w + "x", True)
+        iota(T[w][:, 963:L + 3], [[0, L - 960]], 0, 0, w + "y", True)
 
     unnamed("W")
     op("v", lambda: V.memset(T.et[:, 0:1024], 0.0), [], ["etz"])
@@ -166,8 +177,8 @@ def rank_program(g, core, T, topo):
     ts(T.pp[:, 64:96], T.dd[:], 2, None, A.is_ge, None, ["dd"], ["p2"])
     ts(T.sm[:, 2:3], T.dd[:, 16:17], 2, UP, A.is_equal, A.mult, ["dd"], ["m1"])
     ts(T.sm[:, 3:4], T.dd[:, 16:17], 1, None, A.is_ge, None, ["dd"], ["m2"])
-    ts(T.sm[:, 0:1], T.kk[:, 0:1], 15, None, A.is_equal, None, ["kk"], ["c1"])
-    ts(T.sm[:, 1:2], T.kk[:, 0:1], 15, 1.0 / UP, A.is_lt, A.mult, ["kk"], ["c2"])
+    ts(T.sm[:, 0:1], T.kk[:, 0:1], 15, UP, A.is_equal, A.mult, ["kk"], ["c1"])
+    ts(T.sm[:, 1:2], T.kk[:, 0:1], 15, None, A.is_lt, None, ["kk"], ["c2"])
     ts(T.k20[:], T.kk[:], 20, None, A.mult, None, ["kk"], ["k20"])
     tt(T.pp[:, 96:128], T.pp[:, 32:64], T.pp[:, 64:96], A.add, ["p1", "p2"], ["p12"])
     tt(T.sm[:, 4:5], T.sm[:, 2:3], T.sm[:, 3:4], A.max, ["m1", "m2"], ["m3"])
@@ -178,18 +189,20 @@ def rank_program(g, core, T, topo):
     cpv(T.M[:, 0:16], T.pp[:, 128:144], ["pm"], ["Ma"])
     cpv(T.lc[:, 1:21], T.cc[:], ["cc"], ["lc1"])
     cpv(T.lc[:, 0:1], T.k20[:, 0:1], ["k20"], ["lc0"])
+    ts(T.sm[:, 6:7], T.sm[:, 5:6], 1.0 / UP, None, A.mult, None, ["cp"], ["cq"])
     ts(T.qq[:], T.ee[:], -9.5, 0.05, A.add, A.mult, ["ee"], ["qq"])
     ts(T.rr[:, 0:20], T.ee[:], -16.0, 304.0, A.mult, A.add, ["ee"], ["r1"])
     ts(T.rr[:, 20:40], T.qq[:], 321.0, None, A.mult, None, ["qq"], ["r2"])
     tt(T.rr[:, 40:60], T.rr[:, 0:20], T.rr[:, 20:40], A.add, ["r1", "r2"], ["r3"])
     cpv(T.rho[:], T.rr[:, 40:60], ["r3"], ["rho"])
     CP = T.sm[:, 5:6]
+    CQ = T.sm[:, 6:7]
     for b in range(4):
         cpa(T.et[:, 512 * b + b:512 * b + 512:4], T.dg[:], ["dg", "etz", "ety"], ["et%d" % b])
     cpa(T.M[:, 16:336], T.pp[:, 144:160].indirect(T.lk[:]), ["pm", "lk"], ["Mb"])
     cpv(T.ls[:], T.sti[:], ["sti"], ["ls"])
-    cpa(T.NR[:], T.idn[:].indirect(T.ls[:]), ["idn", "ls"], ["NRa", "NRb"])
-    cpa(T.G1[:, :], T.NR[:].indirect(T.lc[:, 0:21]), ["NRa", "NRb", "lc0", "lc1"], ["G1a", "G1b"])
+    small("a", T.fin[:], T.idn[:].indirect(T.ls[:]), 0, ["idn", "ls"], ["fin"])
+    cpa(T.G1[:, :], T.fin[:].indirect(T.lc[:, 0:21]), ["fin", "lc0", "lc1"], ["G1a", "G1b"])
     quant(T.eq[:], T.es[:], T.et[:], ["et0", "et1", "et2", "et3", "etz", "ety"], ["eq"])
     tt(T.M[:, 16:17], T.sm[:, 4:5], T.pp[:, 16:17], A.max, ["m3", "p0"], ["Mb"])
 
@@ -232,50 +245,49 @@ def rank_program(g, core, T, topo):
     row("G1", "E1")
     offsets("E1", "sc", 1)
     send_state(0)
-    cpa(T.W6[:, 3:961:3], T.idn[:].indirect(T.la[:]), ["idn", "la"], ["W60"])
-    cpa(T.W6[:, 4:962:3], T.idn[:].indirect(T.lb[:]), ["idn", "lb"], ["W61"])
+    small("a", T.W6[:, 3:961:3], T.idn[:].indirect(T.la[:]), 0, ["idn", "la"], ["W60"])
+    small("a", T.W6[:, 4:962:3], T.idn[:].indirect(T.lb[:]), 0, ["idn", "lb"], ["W61"])
     W6K = ["W60", "W61", "W62", "W6x", "W6y", "W63", "W64", "W65"]
     WK = ["W0", "W1", "W2", "W3", "W4a1", "W4b1", "W5", "Wx", "Wy"]
-    less = BIG + BIG // L
     ts(T.tt[:], T.ps4[:, 0:C], 0.0, float(L), A.is_gt, A.mult, ["ps4"], ["tt"])
     plus(T.pk[:], T.tt[:], T.b0[:], ["tt", "b0"], ["pk"])
 
     for r in range(3):
         rid, pid, mask, ne = partner(r)
         rq, rp, sn, pl, xn = [n + str(r) for n in ("rq", "rp", "sn", "pl", "xn")]
-        cpa(T.W[:, 3:961:3], T.pk[:].indirect(T.la[:]), ["pk", "la"], ["W0"])
-        cpv(T.G0[:, :], T.pk[:].indirect(T.sc[:, 0:21]), ["pk", "scm", "scd"], ["G0a", "G0b"])
-        cpv(T.W[:, 4:962:3], T.pk[:].indirect(T.lb[:]), ["pk", "lb"], ["W1"])
+        small("a", T.W[:, 3:961:3], T.pk[:].indirect(T.la[:]), BIG + MID, ["pk", "la"], ["W0"])
+        small("v", T.G0[:, :], T.pk[:].indirect(T.sc[:, 0:21]), BIG + MID, ["pk", "scm", "scd"], ["G0a", "G0b"])
+        small("v", T.W[:, 4:962:3], T.pk[:].indirect(T.lb[:]), BIG + MID, ["pk", "lb"], ["W1"])
         cpa(T.W[:, 5:963:3], T.W[:, 3:961:3], ["W0"], ["W2"])
-        cpg(T.W[:, 2051:3009:3], T.W[:, 3:961:3], ["W0"], ["W3"])
-        cpa(T.W[:, 2053:3011:3], T.W[:, 3:961:3], ["W0"], ["W5"])
+        cpg(T.W[:, L + 3:L + 961:3], T.W[:, 3:961:3], ["W0"], ["W3"])
+        cpa(T.W[:, L + 5:L + 963:3], T.W[:, 3:961:3], ["W0"], ["W5"])
         row("G0", "E0")
-        cpv(T.W[:, 2052:2530:3], T.W[:, 4:482:3], ["W1"], ["W4a1"])
-        cpa(T.W[:, 2532:3010:3], T.W[:, 484:962:3], ["W1"], ["W4b1"])
-        offsets("E0", "o0", less)
+        cpv(T.W[:, L + 4:L + 482:3], T.W[:, 4:482:3], ["W1"], ["W4a1"])
+        cpa(T.W[:, L + 484:L + 962:3], T.W[:, 484:962:3], ["W1"], ["W4b1"])
+        offsets("E0", "o0", -MID)
         if r == 0:
             unnamed("W6")
             cpg(T.W6[:, 5:963:3], T.W6[:, 3:961:3], ["W60"], ["W62"])
-            cpg(T.W6[:, 2051:3009:3], T.W6[:, 3:961:3], ["W60"], ["W63"])
-            cpg(T.W6[:, 2052:3010:3], T.W6[:, 4:962:3], ["W61"], ["W64"])
-            cpg(T.W6[:, 2053:3011:3], T.W6[:, 3:961:3], ["W60"], ["W65"])
+            cpg(T.W6[:, L + 3:L + 961:3], T.W6[:, 3:961:3], ["W60"], ["W63"])
+            cpg(T.W6[:, L + 4:L + 962:3], T.W6[:, 4:962:3], ["W61"], ["W64"])
+            cpg(T.W6[:, L + 5:L + 963:3], T.W6[:, 3:961:3], ["W60"], ["W65"])
             iota(T.b4[:], [[1, C]], BIG, 0, "b4", True)
         gaps = [(T["t%d" % b][:], T["ps%d" % b][:, 0:C], ["ps%d" % b], ["t%d" % b], b) for b in range(4)]
         gaps += [(T["w%d" % b][:], T["ps%d" % b][:, 0:C], ["ps%d" % b], ["w%d" % b], None) for b in range(2)]
         for n in range(1, STAGES + 1):
             o, G, E, on = "o%d" % ((n + 1) % 2), "G%d" % (n % 2), "E%d" % (n % 2), "o%d" % (n % 2)
-            win, wk = (T.W, WK) if n < STAGES else (T.W6, W6K)
-            cpv(T[G][:, 0:16 * CUT], win[:, 0:3011].indirect(T[o][:, 0:CUT]), wk + [o + "m", o + "d"], [G + "a"])
-            cpa(T[G][:, 16 * CUT:336], win[:, 0:3011].indirect(T[o][:, CUT:21]), wk + [o + "m"], [G + "b"])
+            win, wk, G = (T.W, WK, G) if n < STAGES else (T.W6, W6K, "G6")
+            cpv(T[G][:, 0:16 * CUT], win[:, 0:WIN].indirect(T[o][:, 0:CUT]), wk + [o + "m", o + "d"], [G + "a"])
+            cpa(T[G][:, 16 * CUT:336], win[:, 0:WIN].indirect(T[o][:, CUT:21]), wk + [o + "m"], [G + "b"])
             if n < STAGES:
                 for out, in_, rd, wr, b in [gaps.pop(0) for i in range(2 if n == 1 else 1)]:
                     cpa(out, in_, rd, wr)
                     if b is not None:
                         unpack(b, rq, rp)
                 row(G, E)
-                offsets(E, on, less)
-        cpv(T.NR[:, 0:160], T.G0[:, 16:336].indirect(T.rho[:, 0:10]), ["G0a", "G0b", "rho"], ["NRa"])
-        cpa(T.NR[:, 160:320], T.G0[:, 16:336].indirect(T.rho[:, 10:20]), ["G0a", "G0b", "rho"], ["NRb"])
+                offsets(E, on, -MID)
+        cpv(T.NR[:, 0:160], T.G6[:, 16:336].indirect(T.rho[:, 0:10]), ["G6a", "G6b", "rho"], ["NRa"])
+        cpa(T.NR[:, 160:320], T.G6[:, 16:336].indirect(T.rho[:, 10:20]), ["G6a", "G6b", "rho"], ["NRb"])
         if r == 0:
             cpa(T.M0[:], T.pp[:, 112:128].indirect(T.lk[:]), ["p12", "lk"], ["M0"])
         scan(T.EN[:], T.M[:, 16:336], T.NR[:], 0.0, A.mult, A.add, ["NRa", "NRb", "Mb"], ["EN"])
@@ -294,14 +306,14 @@ def rank_program(g, core, T, topo):
         for b in range(4):
             mm(b, T.wq[:, 128 * b:128 * b + 128], T.wp[:, 128 * b:128 * b + 128], T.zq[:], T.zp[:], ["wq", "wp", "zq"])
         if r < 2:
-            row("G0", "E1")
+            row("G6", "E1")
             offsets("E1", "sc", 1)
         if r == 0:
             quant(T.vq[:], T.vs[:], T.vi[:], ["vi"], ["vq"])
         if r == 2:
             ts(T.x320[:], T.x12[:], 320.0, None, A.mult, None, ["x12"], ["x320"])
             plus(T.b4s[:], T.x320[:], T.b4[:], ["x320", "b4"], ["b4s"])
-            op("a", lambda: S.activation(T.ob[:, 0:320], T.NR[:], ACT.Identity, bias=-1.0), ["NRa", "NRb"], ["obs"])
+            op("a", lambda: S.activation(T.ob[:, 0:320], T.NR[:], ACT.Identity, bias=-1.0, scale=UP), ["NRa", "NRb"], ["obs"])
             store("ops", T.op[:, 0:320], T.ob[0:128:16, 0:320], ["obs"])
         for b in range(4):
             hb, pb = T["h%d" % b], T["ps%d" % b]
@@ -340,11 +352,11 @@ def rank_program(g, core, T, topo):
     store("y", T.y[:, :], T.yb[:], ["yb"])
     ts(T.g3[:], T.ps5[:, 0:C], 0.0, 320.0, A.is_gt, A.mult, ["ps5"], ["g3"])
     plus(T.fin[:], T.g3[:], T.b4s[:], ["g3", "b4s"], ["fin"])
-    scan(T.EN[:], T.M0[:], T.fin[:], 0.0, A.mult, A.add, ["fin", "M0"], ["EN"])
-    ts(T.lfa[:], T.EN[:, 15:320:16], CP, -float(BIG), A.mult, A.add, ["EN", "cp"], ["lfa"])
-    ts(T.lfb[:], T.EN[:, 15:320:16], CP, 320.0 - BIG, A.mult, A.add, ["EN", "cp"], ["lfb"])
+    scan(T.tt[:], T.M0[:], T.fin[:], 0.0, A.mult, A.add, ["fin", "M0"], ["tt"])
+    ts(T.lfa[:], T.tt[:, 15:320:16], CQ, -float(BIG), A.mult, A.add, ["tt", "cq"], ["lfa"])
+    ts(T.lfb[:], T.tt[:, 15:320:16], CQ, 320.0 - BIG, A.mult, A.add, ["tt", "cq"], ["lfb"])
     w4 = ["W4a", "W4b", "W4c", "W4d"]
-    op("a", lambda: S.activation(T.ob[:, 320:640], T.W4[:, :].indirect(T.lfa[:]), ACT.Identity, bias=-1.0), w4 + ["lfa"], ["oba"])
-    ts(T.ob[:, 640:960], T.W4[:, :].indirect(T.lfb[:]), -1.0, None, A.add, None, w4 + ["lfb"], ["obb"])
+    op("a", lambda: S.activation(T.ob[:, 320:640], T.W4[:, :].indirect(T.lfa[:]), ACT.Identity, bias=-1.0, scale=UP), w4 + ["lfa"], ["oba"])
+    ts(T.ob[:, 640:960], T.W4[:, :].indirect(T.lfb[:]), UP, -1.0, A.mult, A.add, w4 + ["lfb"], ["obb"])
     store("opt", T.op[:, 320:960], T.ob[0:128:16, 320:960], ["oba", "obb"])
     learn("g", [(s, n) for s, n in count.items()])

@@ -5,9 +5,14 @@ C, STAGES = 320, 6
 L = 1536
 BIG = 4096
 UP = 2.0 ** 24
-MID = 482
-WIN = L + 963
-CUT = 10
+MID = 480
+WIN = L + 3 * C
+NC = 20 + STAGES
+CHAINS = [(0, 14), (14, 26)]
+SHARE = [0, 0]
+EARLY = [1, 2, 2]
+FIRST = 12
+HALF = 192
 SCRATCH = {}
 
 
@@ -17,34 +22,39 @@ def _declare(names, where, cols, dtype):
 
 
 F8, U8 = "float8_e4m3fn_x4", "uint8"
-_declare("sti tai tbi kp kk k20 e16 ee qq ic cc", "sbuf", 20, "int32")
-_declare("d32 dd", "sbuf", 32, "int32")
+_declare("sti qq e16", "sbuf", 20, "int32")
+_declare("tab tq", "sbuf", 40, "int32")
+_declare("lci lq", "sbuf", NC, "int32")
+_declare("kp kk", "sbuf", NC + 2, "int32")
+_declare("d16 dd", "sbuf", 16, "int32")
 _declare("lui", "sbuf", 8, "int32")
 _declare("lu", "sbuf", 8, "uint16")
-_declare("lk rho la lb ls lfa lfb sn0 sn1 sn2 pl0 pl1 pl2", "sbuf", 20, "uint16")
-_declare("lc o0 o1 sc", "sbuf", 22, "uint16")
-_declare("rr", "sbuf", 60, "float32")
-_declare("pp", "sbuf", 160, "float32")
+_declare("lk", "sbuf", NC + 2, "uint16")
+_declare("rho ls lfa lfb pl0 pl1 pl2 pn", "sbuf", 20, "uint16")
+_declare("lab lpos", "sbuf", 40, "uint16")
+_declare("lc o0 o1 sc sn0 sn1 sn2", "sbuf", NC, "uint16")
+_declare("rr pp bl ra", "sbuf", 64, "float32")
+_declare("rt", "sbuf", 120, "float32")
 _declare("sm", "sbuf", 8, "float32")
-_declare("G6", "sbuf", 336, "float32")
-_declare("M", "sbuf", 336, "bfloat16")
-_declare("G0 G1 E0 E1", "sbuf", 336, "float16")
-_declare("NR EN", "sbuf", C, "float16")
-_declare("M0 idn b0 b4 uu b4s g1 g2 g3 x12 x320 fin tt pk yb", "sbuf", C, "float32")
-_declare("W W6", "sbuf", WIN + 5, "float32")
+_declare("M", "sbuf", 16 * (NC + 2), "bfloat16")
+_declare("G0 G1", "sbuf", 16 * NC, "float16")
+_declare("E0 E1", "sbuf", 16 * (NC + len(CHAINS)), "float16")
+_declare("NR EN X16", "sbuf", C, "float16")
+_declare("G6 nat b0 b0p uu g1 g2 x12 fin tt pk yb", "sbuf", C, "float32")
+_declare("W W6", "sbuf", WIN, "float32")
 _declare("W4", "sbuf", 1280, "float32")
 _declare("ob", "sbuf", 960, "float32")
-_declare("one dg", "sbuf", 128, "bfloat16")
+_declare("one", "sbuf", 128, "bfloat16")
 _declare("ui vi", "sbuf", 512, "bfloat16")
-_declare("et", "sbuf", 2048, "bfloat16")
+_declare("et", "sbuf", 516, "bfloat16")
 _declare("xi ht z za xn0 xn1 xn2", "sbuf", 4 * C, "bfloat16")
 _declare("t0 t1 t2 t3 w0 w1 w2 w3 h0 h1 h2 h3", "sbuf", C, "bfloat16")
-for _q, _p, _n in (("wq", "wp", 512), ("uq", "us", 128), ("urq", "urs", 128), ("vq", "vs", 128), ("eq", "es", 512), ("hq", "hp", C), ("zq", "zp", C)):
+for _q, _p, _n in (("wq", "wp", 512), ("uq", "us", 128), ("urq", "urs", 128), ("vq", "vs", 128), ("eq", "es", 512), ("hq", "hp", C), ("zq", "zp", C), ("iq", "ip", C)):
     _declare(_q, "sbuf", _n, F8)
     _declare(_p, "sbuf", _n, U8)
 _declare("rq0 rq1 rq2 xq0 xq1 xq2 xq3", "sbuf", C, F8)
 _declare("rp0 rp1 rp2 xs0 xs1 xs2 xs3", "sbuf", C, U8)
-_declare("ps0 ps1 ps2 ps3 ps4 ps5 ps6", "psum", 512, "float32")
+_declare("ps0 ps1 ps2 ps3 ps4 ps5 ps6 ps7", "psum", 512, "float32")
 SEMAPHORES = ("cv ct ca cg sent gotl0 gotl1 gotl2 gotz0 gotz1 gotz2 ld_st ld_x ld_ta ld_tb ld_u ld_wc ld_ws ld_v "
               "sv_y sv_ops sv_opt sv_oc sv_os0 sv_os1 sv_os2 sv_os3").split()
 
@@ -93,6 +103,9 @@ def rank_program(g, core, T, topo):
 
     V, S, P = g.vector, g.scalar, g.tensor
 
+    def keys(name, lo, hi):
+        return ["%s:%d" % (name, i) for i in range(lo, hi)]
+
     def load(q, name, out, in_, key):
         op(q, lambda: queues[q].dma_start(out, in_), [], [key], sem="ld_" + name, inc=16)
 
@@ -105,8 +118,8 @@ def rank_program(g, core, T, topo):
         else:
             op("g", lambda: g.iota(out, pattern, base, cm), [], [wr])
 
-    def cpg(out, in_, rd, wr):
-        op("g", lambda: g.affine_select(out, in_, [[1, C]], A.is_ge, 0.0, 0, 0), rd, wr)
+    def cpg(out, in_, rd, wr, n=C):
+        op("g", lambda: g.affine_select(out, in_, [[1, n]], A.is_ge, 0.0, 0, 0), rd, wr)
 
     def ts(out, in0, s1, s2, o0, o1, rd, wr):
         if o1 is None:
@@ -123,14 +136,20 @@ def rank_program(g, core, T, topo):
     def cpa(out, in_, rd, wr):
         op("a", lambda: S.activation(out, in_, ACT.Copy), rd, wr)
 
-    def small(q, out, in_, less, rd, wr):
+    def cp(q, out, in_, rd, wr):
+        (cpv if q == "v" else cpa)(out, in_, rd, wr)
+
+    def scaled(q, out, in_, scale, bias, rd, wr):
         if q == "a":
-            op("a", lambda: S.activation(out, in_, ACT.Identity, bias=-less / UP, scale=1.0 / UP), rd, wr)
+            op("a", lambda: S.activation(out, in_, ACT.Identity, bias=float(bias), scale=float(scale)), rd, wr)
         else:
-            ts(out, in_, -float(less), 1.0 / UP, A.add, A.mult, rd, wr)
+            ts(out, in_, float(scale), float(bias), A.mult, A.add, rd, wr)
 
     def scan(out, d0, d1, init, o0, o1, rd, wr):
         op("v", lambda: V.tensor_tensor_scan(out, d0, d1, init, o0, o1), rd, wr)
+
+    def pick(out, row, n, rd, wr, first=0):
+        scan(out, T.M[:, first:first + n], row, 0.0, A.mult, A.add, rd + ["M"], wr)
 
     def plus(out, a, b, rd, wr):
         scan(out, a, b, float(BIG), A.min, A.add, rd, wr)
@@ -138,92 +157,69 @@ def rank_program(g, core, T, topo):
     def quant(codes, plane, tile, rd, wr):
         op("v", lambda: V.quantize_mx(codes, plane, tile), rd, wr)
 
-    def mm(bank, lq, lp, rq, rp, rd):
-        op("t", lambda: P.matmul_mx(T["ps%d" % bank][:, 0:C], lq, lp, rq, rp, True, True), rd, ["ps%d" % bank])
+    def mm(bank, lq, lp, rq, rp, rd, n=C):
+        op("t", lambda: P.matmul_mx(T["ps%d" % bank][:, 0:n], lq, lp, rq, rp, True, True), rd, ["ps%d" % bank])
 
-    load("y", "st", T.sti[:], T.st[:], "sti")
-    load("y", "x", T.xi[:], T.x[:], "xi")
+    CP = T.sm[:, 0:1]
+    CN = T.sm[:, 1:2]
+    CQ = T.sm[:, 2:3]
+
     load("a", "u", T.ui[:], T.u[:], "ui")
-    load("a", "ta", T.tai[:], T.ta[:], "tai")
-    load("y", "tb", T.tbi[:], T.tb[:], "tbi")
+    load("y", "x", T.xi[:], T.x[:], "xi")
+    load("y", "st", T.sti[:], T.st[:], "sti")
+    load("a", "ta", T.tab[:, 0:20], T.ta[:], "ta")
+    load("y", "tb", T.tab[:, 20:40], T.tb[:], "tb")
     learn("y", wrote["xi"])
     load("y", "wc", T.wq[:, :].bitcast(dt.uint8), T.wc[:, :], "wq")
     load("y", "ws", T.wp[:, :], T.ws[:, :], "wp")
     load("y", "v", T.vi[:], T.v[:], "vi")
 
+    def slot(w, k, lo=0, hi=C):
+        first = k % 3 + L * (k // 3)
+        return T[w][:, first + 3 * lo:first + 3 * hi - 2:3]
+
+    IDN, POS = T.W[:, 3 * C:4 * C], T.W6[:, 3 * C:4 * C]
     op("v", lambda: V.memset(T.one[:], 1.0), [], ["one"])
-    iota(T.kp[:], [[0, 20]], 0, 1, "kp")
-    iota(T.d32[:], [[1, 2], [1, 16]], 127, -1, "d32")
+    op("v", lambda: V.memset(T.et[:, :], 0.0), [], ["et"])
+    iota(T.d16[:], [[1, 16]], 128, -1, "d16")
+    iota(T.kp[:], [[0, NC + 2]], 0, 1, "kp")
+    iota(T.lci[:], [[-1, NC]], NC - 1, 20, "lci")
     iota(T.lui[:], [[16, 8]], 0, 0, "lui")
-    op("g", lambda: g.affine_select(T.dg[:], T.one[:], [[-1, 128]], A.is_equal, 0.0, 0, 1), ["one"], ["dg"])
-    iota(T.ic[:], [[-1, 20]], 19, 0, "ic")
-    iota(T.e16[:], [[16, 20]], 0, 0, "e16")
-    iota(T.idn[:], [[1, C]], 1, 0, "idn", True)
-    iota(T.b0[:], [[3, C]], 3 + BIG, 0, "b0", True)
-
-    def unnamed(w):
-        iota(T[w][:, 0:3], [[0, 3]], 0, 0, w + "x", True)
-        iota(T[w][:, 963:L + 3], [[0, L - 960]], 0, 0, w + "y", True)
-
-    unnamed("W")
-    op("v", lambda: V.memset(T.et[:, 0:1024], 0.0), [], ["etz"])
-    cpa(T.et[:, 1024:2048], T.et[:, 0:1024], ["etz"], ["ety"])
+    iota(T.W[:, 3 * C:L], [[1, L - 3 * C]], 1, 0, "idn", True)
+    op("g", lambda: g.affine_select(T.et[:, 3:515:4], T.one[:], [[-1, 128]], A.is_equal, 0.0, 0, 1), ["one"], ["et"])
+    iota(T.W6[:, 3 * C:L + 4], [[1, 29], [-16, 20]], 304 + 1, 0, "pos", True)
+    ts(T.dd[:], T.d16[:], 15, None, A.bitwise_and, None, ["d16"], ["dd"])
     ts(T.kk[:], T.kp[:], 15, None, A.bitwise_and, None, ["kp"], ["kk"])
-    ts(T.dd[:], T.d32[:], 15, None, A.bitwise_and, None, ["d32"], ["dd"])
+    ts(T.pp[:, 0:16], T.dd[:], 1, UP, A.is_equal, A.mult, ["dd"], ["p0"])
+    ts(T.pp[:, 16:32], T.dd[:], 1, 1.0 / UP / L, A.is_ge, A.max, ["dd"], ["p1"])
+    ts(T.lq[:], T.lci[:], -159.5, 1.0 / C, A.add, A.mult, ["lci"], ["lq"])
     cpv(T.lk[:], T.kk[:], ["kk"], ["lk"])
+    tt(T.pp[:, 32:48], T.pp[:, 0:16], T.pp[:, 16:32], A.max, ["p0", "p1"], ["pm"])
     cpv(T.lu[:], T.lui[:], ["lui"], ["lu"])
-    ts(T.pp[:, 0:32], T.dd[:], 0, 1.0 / UP / L, A.is_equal, A.mult, ["dd"], ["p0"])
-    ts(T.pp[:, 32:64], T.dd[:], 1, UP, A.is_equal, A.mult, ["dd"], ["p1"])
-    ts(T.pp[:, 64:96], T.dd[:], 2, None, A.is_ge, None, ["dd"], ["p2"])
-    ts(T.sm[:, 2:3], T.dd[:, 16:17], 2, UP, A.is_equal, A.mult, ["dd"], ["m1"])
-    ts(T.sm[:, 3:4], T.dd[:, 16:17], 1, None, A.is_ge, None, ["dd"], ["m2"])
-    ts(T.sm[:, 0:1], T.kk[:, 0:1], 15, UP, A.is_equal, A.mult, ["kk"], ["c1"])
-    ts(T.sm[:, 1:2], T.kk[:, 0:1], 15, None, A.is_lt, None, ["kk"], ["c2"])
-    ts(T.k20[:], T.kk[:], 20, None, A.mult, None, ["kk"], ["k20"])
-    tt(T.pp[:, 96:128], T.pp[:, 32:64], T.pp[:, 64:96], A.add, ["p1", "p2"], ["p12"])
-    tt(T.sm[:, 4:5], T.sm[:, 2:3], T.sm[:, 3:4], A.max, ["m1", "m2"], ["m3"])
-    tt(T.sm[:, 5:6], T.sm[:, 0:1], T.sm[:, 1:2], A.add, ["c1", "c2"], ["cp"])
-    tt(T.pp[:, 128:160], T.pp[:, 96:128], T.pp[:, 0:32], A.add, ["p12", "p0"], ["pm"])
-    tt(T.cc[:], T.k20[:], T.ic[:], A.add, ["k20", "ic"], ["cc"])
-    tt(T.ee[:], T.e16[:], T.kk[:], A.add, ["e16", "kk"], ["ee"])
-    cpv(T.M[:, 0:16], T.pp[:, 128:144], ["pm"], ["Ma"])
-    cpv(T.lc[:, 1:21], T.cc[:], ["cc"], ["lc1"])
-    cpv(T.lc[:, 0:1], T.k20[:, 0:1], ["k20"], ["lc0"])
-    ts(T.sm[:, 6:7], T.sm[:, 5:6], 1.0 / UP, None, A.mult, None, ["cp"], ["cq"])
-    ts(T.qq[:], T.ee[:], -9.5, 0.05, A.add, A.mult, ["ee"], ["qq"])
-    ts(T.rr[:, 0:20], T.ee[:], -16.0, 304.0, A.mult, A.add, ["ee"], ["r1"])
-    ts(T.rr[:, 20:40], T.qq[:], 321.0, None, A.mult, None, ["qq"], ["r2"])
-    tt(T.rr[:, 40:60], T.rr[:, 0:20], T.rr[:, 20:40], A.add, ["r1", "r2"], ["r3"])
-    cpv(T.rho[:], T.rr[:, 40:60], ["r3"], ["rho"])
-    CP = T.sm[:, 5:6]
-    CQ = T.sm[:, 6:7]
-    for b in range(4):
-        cpa(T.et[:, 512 * b + b:512 * b + 512:4], T.dg[:], ["dg", "etz", "ety"], ["et%d" % b])
-    cpa(T.M[:, 16:336], T.pp[:, 144:160].indirect(T.lk[:]), ["pm", "lk"], ["Mb"])
+    ts(T.rr[:, 0:NC], T.lq[:], -float(C), None, A.mult, None, ["lq"], ["r0"])
+    ts(T.sm[:, 0:1], T.dd[:, 0:1], 1, UP, A.is_equal, A.mult, ["dd"], ["c0"])
+    ts(T.sm[:, 1:2], T.dd[:, 0:1], 2, UP, A.is_equal, A.mult, ["dd"], ["c1"])
+    ts(T.sm[:, 2:3], T.dd[:, 0:1], 1, 1.0 / UP, A.not_equal, A.max, ["dd"], ["cq"])
+    tt(T.rr[:, 32:32 + NC], T.rr[:, 0:NC], T.lci[:], A.add, ["r0", "lci"], ["r1"])
+    cpa(T.M[:, :], T.pp[:, 32:48].indirect(T.lk[:, :]), ["pm", "lk"], ["M"])
+    ts(T.sm[:, 0:2], T.sm[:, 0:2], 1.0, None, A.max, None, ["c0", "c1"], ["cp"])
     cpv(T.ls[:], T.sti[:], ["sti"], ["ls"])
-    small("a", T.fin[:], T.idn[:].indirect(T.ls[:]), 0, ["idn", "ls"], ["fin"])
-    cpa(T.G1[:, :], T.fin[:].indirect(T.lc[:, 0:21]), ["fin", "lc0", "lc1"], ["G1a", "G1b"])
-    quant(T.eq[:], T.es[:], T.et[:], ["et0", "et1", "et2", "et3", "etz", "ety"], ["eq"])
-    tt(T.M[:, 16:17], T.sm[:, 4:5], T.pp[:, 16:17], A.max, ["m3", "p0"], ["Mb"])
-
+    cpv(T.lc[:], T.rr[:, 32:32 + NC], ["r1"], ["lc"])
+    scaled("a", T.fin[:], IDN.indirect(T.ls[:]), 1 / UP, 0, ["idn", "ls"], ["fin"])
     quant(T.uq[:], T.us[:], T.ui[:], ["ui"], ["uq"])
+    cpv(T.lab[:], T.tab[:], ["ta", "tb"], ["lab"])
     cpv(T.urq[:, 0:128].bitcast(dt.uint32), T.uq[:, 0:128].bitcast(dt.uint32).indirect(T.lu[:, 0:8]), ["uq", "lu"], ["urq"])
     cpa(T.urs[:, 0:128], T.us[:, 0:128].indirect(T.lu[:, 0:8]), ["uq", "lu"], ["urs"])
-    cpv(T.la[:], T.tai[:], ["tai"], ["la"])
-    cpv(T.lb[:], T.tbi[:], ["tbi"], ["lb"])
+    cpa(T.G1[:, :], T.fin[:].indirect(T.lc[:, :]), ["fin", "lc"], keys("G1", 0, NC))
 
-    def scores(r):
-        mm(4, T.urq[:], T.urs[:], T["xq%d" % r][:], T["xs%d" % r][:], ["urq", "urs", "xq%d" % r])
+    def scores(q, p):
+        mm(4, T.urq[:], T.urs[:], T[q][:], T[p][:], ["urq", "urs", q])
 
     def unpack(b, q, p):
-        mm(b, T.eq[:, 128 * b:128 * b + 128], T.es[:, 128 * b:128 * b + 128], T[q][:], T[p][:], ["eq", q])
+        mm(b, T.eq[:, 128 * b:128 * b + 128], T.es[:, 128 * b:128 * b + 128], T[q][:], T[p][:], ["eq%d" % b, q, p])
 
-    def row(G, E):
-        scan(T[E][:, :], T.M[:, :], T[G][:, :], 0.0, A.mult, A.add, [G + "a", G + "b", "Ma", "Mb"], [E])
-
-    def offsets(E, o, less):
-        ts(T[o][:, 1:21], T[E][:, 31:336:16], CP, -float(less), A.mult, A.add, [E, "cp"], [o + "m"])
-        ts(T[o][:, 0:1], T[E][:, 335:336], CP, -float(less), A.mult, A.add, [E, "cp"], [o + "d"])
+    def unit(b):
+        quant(T.eq[:, 128 * b:128 * b + 128], T.es[:, 128 * b:128 * b + 128], T.et[:, 3 - b:515 - b], ["et"], ["eq%d" % b])
 
     def partner(r):
         other = T.cores[rank ^ STEP[r]]
@@ -232,117 +228,218 @@ def rank_program(g, core, T, topo):
     def send_state(r):
         rid, pid, mask, ne = partner(r)
         xq, xs, rq, rp, sem = [n + str(r) for n in ("xq", "xs", "rq", "rp", "gotz")]
-        learn("g", wrote[xq])
+        learn("g", wrote[xq] + wrote.get(xs, []))
         g.remote_dma(T[rq][:, :].bitcast(dt.uint8), T[xq][:, :].bitcast(dt.uint8), T.sem[sem], T.sem.sent, pid, rid, mask)
         g.remote_dma(T[rp][:, :], T[xs][:, :], T.sem[sem], T.sem.sent, pid, rid, mask)
         count["sent"] = count.get("sent", 0) + 2 * ne
         wrote[rq] = [(sem, 2 * ne)]
 
-    quant(T.xq0[:], T.xs0[:], T.xi[:], ["xi"], ["xq0"])
-    scores(0)
+    scaled("v", T.b0[:], IDN, 3, BIG - 3, ["idn"], ["b0"])
+    unit(0)
+    unit(1)
+    quant(T.iq[:], T.ip[:], T.xi[:], ["xi"], ["iq"])
+    scores("iq", "ip")
+    pick(T.E1[:, 0:16 * NC], T.G1[:, :], 16 * NC, keys("G1", 0, NC), keys("E1", 0, NC))
+    cpv(T.xq0[:, :].bitcast(dt.uint32), T.iq[:, :].bitcast(dt.uint32).indirect(T.lc[:, STAGES:NC]), ["iq", "lc"], ["xq0"])
+    cpa(T.xs0[:, :], T.ip[:, :].indirect(T.lc[:, STAGES:NC]), ["iq", "lc"], ["xs0"])
+    send_state(0)
+    ts(T.tt[:], T.ps4[:, 0:C], 0.0, float(L), A.is_gt, A.mult, ["ps4"], ["tt"])
+    ts(T.sc[:, :], T.E1[:, 15:16 * NC:16], CP, -1.0, A.mult, A.add, keys("E1", 0, NC) + ["cp"], keys("sc", 0, NC))
+    unit(2)
+    plus(T.pk[:], T.tt[:], T.b0[:], ["tt", "b0"], ["pk"])
+    unit(3)
     for b in range(4):
         unpack(b, "xq0", "xs0")
-    row("G1", "E1")
-    offsets("E1", "sc", 1)
-    send_state(0)
-    small("a", T.W6[:, 3:961:3], T.idn[:].indirect(T.la[:]), 0, ["idn", "la"], ["W60"])
-    small("a", T.W6[:, 4:962:3], T.idn[:].indirect(T.lb[:]), 0, ["idn", "lb"], ["W61"])
-    W6K = ["W60", "W61", "W62", "W6x", "W6y", "W63", "W64", "W65"]
-    WK = ["W0", "W1", "W2", "W3", "W4a1", "W4b1", "W5", "Wx", "Wy"]
-    ts(T.tt[:], T.ps4[:, 0:C], 0.0, float(L), A.is_gt, A.mult, ["ps4"], ["tt"])
-    plus(T.pk[:], T.tt[:], T.b0[:], ["tt", "b0"], ["pk"])
+    scaled("a", slot("W6", 0), POS.indirect(T.lab[:, 0:20]), 1 / UP, 0, ["pos", "lab"], ["W60"])
+    W6K = ["W60", "W61a", "W61b", "W62", "pos", "W63", "W64", "W65"]
+    WK = ["W0", "W1", "W2", "W3", "W4", "W5", "idn"]
 
     for r in range(3):
         rid, pid, mask, ne = partner(r)
         rq, rp, sn, pl, xn = [n + str(r) for n in ("rq", "rp", "sn", "pl", "xn")]
-        small("a", T.W[:, 3:961:3], T.pk[:].indirect(T.la[:]), BIG + MID, ["pk", "la"], ["W0"])
-        small("v", T.G0[:, :], T.pk[:].indirect(T.sc[:, 0:21]), BIG + MID, ["pk", "scm", "scd"], ["G0a", "G0b"])
-        small("v", T.W[:, 4:962:3], T.pk[:].indirect(T.lb[:]), BIG + MID, ["pk", "lb"], ["W1"])
-        cpa(T.W[:, 5:963:3], T.W[:, 3:961:3], ["W0"], ["W2"])
-        cpg(T.W[:, L + 3:L + 961:3], T.W[:, 3:961:3], ["W0"], ["W3"])
-        cpa(T.W[:, L + 5:L + 963:3], T.W[:, 3:961:3], ["W0"], ["W5"])
-        row("G0", "E0")
-        cpv(T.W[:, L + 4:L + 482:3], T.W[:, 4:482:3], ["W1"], ["W4a1"])
-        cpa(T.W[:, L + 484:L + 962:3], T.W[:, 484:962:3], ["W1"], ["W4b1"])
-        offsets("E0", "o0", -MID)
+        lab, sc = ("lab", "sc") if r == 0 else ("lpos", "sn%d" % (r - 1))
+        small = (1 / UP, -(BIG + MID) / UP)
+        last = r == 2
+
+        def gather(n, lo, hi, q):
+            G, o = "G%d" % (n % 2), "o%d" % ((n + 1) % 2)
+            if n == 0:
+                scaled(q, T.G0[:, 16 * lo:16 * hi], T.pk[:].indirect(T[sc][:, lo:hi]), small[0], small[1], ["pk"] + keys(sc, lo, hi), keys(G, lo, hi))
+            elif n == STAGES and last:
+                cp(q, T.G6[:, 16 * (lo - n):16 * (hi - n)], T.W6[:, 0:WIN].indirect(T[o][:, lo:hi]), W6K + keys(o, lo, hi), keys("G6", lo, hi))
+            else:
+                win, wk = (T.W, WK) if n < STAGES else (T.W6, W6K)
+                cp(q, T[G][:, 16 * lo:16 * hi], win[:, 0:WIN].indirect(T[o][:, lo:hi]), wk + keys(o, lo, hi), keys(G, lo, hi))
+
+        def row(n, lo, hi, i):
+            G, E = "G%d" % (n % 2), "E%d" % (n % 2)
+            pick(T[E][:, 16 * (lo + i):16 * (hi + i)], T[G][:, 16 * lo:16 * hi], 16 * (hi - lo), keys(G, lo, hi), keys(E, lo + i, hi + i))
+
+        def cast(n, lo, hi, i):
+            E = "E%d" % (n % 2)
+            o, more = ("o%d" % (n % 2), MID) if n < STAGES else (sn, -1)
+            ts(T[o][:, lo:hi], T[E][:, 16 * (lo + i) + 15:16 * (hi + i):16], CP, float(more), A.mult, A.add, keys(E, lo + i, hi + i) + ["cp"], keys(o, lo, hi))
+
+        scaled("a", slot("W", 0), T.pk[:].indirect(T[lab][:, 0:20]), small[0], small[1], ["pk", lab], ["W0"])
+        scaled("v", slot("W", 1), T.pk[:].indirect(T[lab][:, 20:40]), small[0], small[1], ["pk", lab], ["W1"])
+        gather(0, 0, FIRST, "v")
+        gather(0, FIRST, NC, "a")
+        cpg(slot("W", 3), slot("W", 0), ["W0"], ["W3"])
+        cpa(slot("W", 2), slot("W", 0), ["W0"], ["W2"])
+        cpv(slot("W", 4), slot("W", 1), ["W1"], ["W4"])
+        cpa(slot("W", 5), slot("W", 0), ["W0"], ["W5"])
+        row(0, 0, NC, 0)
+        cast(0, 0, NC, 0)
+        gaps, fill = [], []
         if r == 0:
-            unnamed("W6")
-            cpg(T.W6[:, 5:963:3], T.W6[:, 3:961:3], ["W60"], ["W62"])
-            cpg(T.W6[:, L + 3:L + 961:3], T.W6[:, 3:961:3], ["W60"], ["W63"])
-            cpg(T.W6[:, L + 4:L + 962:3], T.W6[:, 4:962:3], ["W61"], ["W64"])
-            cpg(T.W6[:, L + 5:L + 963:3], T.W6[:, 3:961:3], ["W60"], ["W65"])
-            iota(T.b4[:], [[1, C]], BIG, 0, "b4", True)
-        gaps = [(T["t%d" % b][:], T["ps%d" % b][:, 0:C], ["ps%d" % b], ["t%d" % b], b) for b in range(4)]
-        gaps += [(T["w%d" % b][:], T["ps%d" % b][:, 0:C], ["ps%d" % b], ["w%d" % b], None) for b in range(2)]
-        for n in range(1, STAGES + 1):
-            o, G, E, on = "o%d" % ((n + 1) % 2), "G%d" % (n % 2), "E%d" % (n % 2), "o%d" % (n % 2)
-            win, wk, G = (T.W, WK, G) if n < STAGES else (T.W6, W6K, "G6")
-            cpv(T[G][:, 0:16 * CUT], win[:, 0:WIN].indirect(T[o][:, 0:CUT]), wk + [o + "m", o + "d"], [G + "a"])
-            cpa(T[G][:, 16 * CUT:336], win[:, 0:WIN].indirect(T[o][:, CUT:21]), wk + [o + "m"], [G + "b"])
-            if n < STAGES:
-                for out, in_, rd, wr, b in [gaps.pop(0) for i in range(2 if n == 1 else 1)]:
-                    cpa(out, in_, rd, wr)
-                    if b is not None:
-                        unpack(b, rq, rp)
-                row(G, E)
-                offsets(E, on, -MID)
-        cpv(T.NR[:, 0:160], T.G6[:, 16:336].indirect(T.rho[:, 0:10]), ["G6a", "G6b", "rho"], ["NRa"])
-        cpa(T.NR[:, 160:320], T.G6[:, 16:336].indirect(T.rho[:, 10:20]), ["G6a", "G6b", "rho"], ["NRb"])
-        if r == 0:
-            cpa(T.M0[:], T.pp[:, 112:128].indirect(T.lk[:]), ["p12", "lk"], ["M0"])
-        scan(T.EN[:], T.M[:, 16:336], T.NR[:], 0.0, A.mult, A.add, ["NRa", "NRb", "Mb"], ["EN"])
-        ts(T[sn][:], T.EN[:, 15:320:16], CP, -1.0, A.mult, A.add, ["EN", "cp"], [sn])
-        learn("g", wrote[sn])
-        g.remote_dma(T[pl][:, :], T[sn][:, :], T.sem["gotl%d" % r], T.sem.sent, pid, rid, mask)
+            for k in (2, 3, 5):
+                cpg(slot("W6", k), slot("W6", 0), ["W60", "pos"], ["W6%d" % k])
+            scaled("a", slot("W6", 1, 0, 160), POS.indirect(T.lab[:, 20:30]), 1 / UP, 0, ["pos", "lab"], ["W61a"])
+
+            def rest():
+                scaled("a", slot("W6", 1, 160, C), POS.indirect(T.lab[:, 30:40]), 1 / UP, 0, ["pos", "lab"], ["W61b"])
+                cpg(slot("W6", 4), slot("W6", 1), ["W61a", "W61b", "pos"], ["W64"])
+                iota(T.b0p[:], [[-3, 20], [60, 16]], 57 + BIG, 0, "b0p", True)
+            gaps.append(rest)
+            fill += [lambda: ts(T.tq[:], T.tab[:], -9.5, 0.05, A.add, A.mult, ["ta", "tb"], ["tq"]),
+                     lambda: ts(T.rt[:, 0:40], T.tab[:], -16.0, 304.0, A.mult, A.add, ["ta", "tb"], ["rt0"]),
+                     lambda: ts(T.rt[:, 40:80], T.tq[:], 321.0, None, A.mult, None, ["tq"], ["rt1"]),
+                     lambda: tt(T.rt[:, 80:120], T.rt[:, 0:40], T.rt[:, 40:80], A.add, ["rt0", "rt1"], ["rt2"]),
+                     lambda: cpv(T.lpos[:], T.rt[:, 80:120], ["rt2"], ["lpos"])]
+        if r == 1:
+            fill += [lambda: pick(T.NR[:], T.X16[:], C, ["X16"], ["NRa", "NRb"]),
+                     lambda: ts(T.rho[:], T.NR[:, 15:C:16], CP, -1.0, A.mult, A.add, ["NRa", "NRb", "cp"], ["rho"]),
+                     lambda: quant(T.vq[:], T.vs[:], T.vi[:], ["vi"], ["vq"]),
+                     lambda: tt(T.qq[:], T.e16[:], T.kk[:, 0:20], A.add, ["e16", "kk"], ["qq"]),
+                     lambda: ts(T.bl[:, 0:20], T.qq[:], CQ, None, A.mult, None, ["qq", "cq"], ["bl0"])]
+        if last:
+            fill += [lambda: pick(T.EN[:], T.X16[:], C, ["X16"], ["EN"]),
+                     lambda: ts(T.bl[:, 20:40], T.EN[:, 15:C:16], CP, 0.5, A.mult, A.is_gt, ["EN", "cp"], ["bl1"]),
+                     lambda: ts(T.bl[:, 20:40], T.bl[:, 20:40], CQ, float(C), A.mult, A.mult, ["bl1", "cq"], ["bl1"]),
+                     lambda: tt(T.bl[:, 40:60], T.bl[:, 20:40], T.bl[:, 0:20], A.add, ["bl0", "bl1"], ["bl2"])]
+
+        def own(b):
+            cpa(T["t%d" % b][:], T["ps%d" % b][:, 0:C], ["ps%d" % b], ["t%d" % b])
+            unpack(b, rq, rp)
+        gaps += [(lambda b=b: own(b)) for b in range(4)]
+        gaps += [(lambda b=b: cpa(T["w%d" % b][:], T["ps%d" % b][:, 0:C], ["ps%d" % b], ["w%d" % b])) for b in range(EARLY[r])]
+        steps = [(n, i) for n in range(1, STAGES + 1) for i in range(2)]
+
+        def span(n, i):
+            return (max(CHAINS[i][0], n - n % 2), CHAINS[i][1])
+
+        for t in range(len(steps) + 1):
+            n, i = steps[t - 1]
+            behind = t > 0 and not (last and n == STAGES)
+            if behind:
+                row(n, span(n, i)[0] - (i if n < STAGES else 0), span(n, i)[1], i)
+            if t < len(steps):
+                lo, hi = span(*steps[t])
+                cut = (lo + hi) // 4 * 2 + SHARE[steps[t][1]]
+                gather(steps[t][0], lo, cut, "v")
+                gather(steps[t][0], cut, hi, "a")
+                if steps[t][1] == 1 and gaps:
+                    gaps.pop(0)()
+            if behind:
+                cast(n, span(min(n + 1, STAGES), i)[0], span(n, i)[1], i)
+            if t > 1 and fill:
+                fill.pop(0)()
+        if last:
+            cpv(T.NR[:, 0:160], T.G6[:, :].indirect(T.rho[:, 0:10]), keys("G6", STAGES, NC) + ["rho"], ["NRa"])
+            cpa(T.NR[:, 160:320], T.G6[:, :].indirect(T.rho[:, 10:20]), keys("G6", STAGES, NC) + ["rho"], ["NRb"])
+            pick(T.EN[:], T.NR[:], C, ["NRa", "NRb"], ["EN"])
+            ts(T[sn][:, STAGES:NC], T.EN[:, 15:C:16], CP, -1.0, A.mult, A.add, ["EN", "cp"], keys(sn, STAGES, NC))
+        snk, SN = keys(sn, STAGES, NC), T[sn][:, STAGES:NC]
+        learn("g", [tok for k in snk for tok in wrote[k]])
+        g.remote_dma(T[pl][:, :], SN, T.sem["gotl%d" % r], T.sem.sent, pid, rid, mask)
         count["sent"] += ne
         wrote[pl] = [("gotl%d" % r, ne)]
-        for b in range(4):
-            (cpv if b < 2 else cpa)(T.z[:, b:4 * C:4], T["t%d" % b][:].indirect(T[sn][:]), ["t%d" % b, sn], ["z%d" % b])
-        for b in range(2, 4):
-            (cpv if b == 2 else cpa)(T["w%d" % b][:], T["ps%d" % b][:, 0:C], ["ps%d" % b], ["w%d" % b])
-        for b in range(4):
-            (cpv if b < 2 else cpa)(T.za[:, b:4 * C:4], T["w%d" % b][:].indirect(T[pl][:]), ["w%d" % b, pl], ["za%d" % b])
-        quant(T.zq[:], T.zp[:], T.za[:], ["za%d" % b for b in range(4)], ["zq"])
-        for b in range(4):
-            mm(b, T.wq[:, 128 * b:128 * b + 128], T.wp[:, 128 * b:128 * b + 128], T.zq[:], T.zp[:], ["wq", "wp", "zq"])
-        if r < 2:
-            row("G6", "E1")
-            offsets("E1", "sc", 1)
         if r == 0:
-            quant(T.vq[:], T.vs[:], T.vi[:], ["vi"], ["vq"])
-        if r == 2:
-            ts(T.x320[:], T.x12[:], 320.0, None, A.mult, None, ["x12"], ["x320"])
-            plus(T.b4s[:], T.x320[:], T.b4[:], ["x320", "b4"], ["b4s"])
-            op("a", lambda: S.activation(T.ob[:, 0:320], T.NR[:], ACT.Identity, bias=-1.0, scale=UP), ["NRa", "NRb"], ["obs"])
-            store("ops", T.op[:, 0:320], T.ob[0:128:16, 0:320], ["obs"])
+            iota(T.nat[:], [[-1, 20], [20, 16]], 19, 0, "nat", True)
+            iota(T.e16[:], [[16, 20]], 0, 0, "e16")
         for b in range(4):
-            hb, pb = T["h%d" % b], T["ps%d" % b]
-            op("a", lambda: S.activation(hb[:], pb[:, 0:C], ACT.Copy, scale=0.03125), ["ps%d" % b], ["h%d" % b])
-            tt(T[xn][:, b:4 * C:4], hb[:].indirect(T[pl][:]), T.z[:, b:4 * C:4], A.add, ["h%d" % b, pl, "z%d" % b], [xn + str(b)])
-        for b in range(4):
-            cpa(T.ht[:, b:4 * C:4], T["h%d" % b][:], ["h%d" % b], ["ht%d" % b])
-        if r == 1:
-            for i, key in enumerate(("W4a", "W4b", "W4c", "W4d")):
-                cpg(T.W4[:, 320 * i:320 * i + 320], T.W6[:, 3 + i % 2:961 + i % 2:3], ["W6%d" % (i % 2)], [key])
-        xq, xs = "xq%d" % (r + 1), "xs%d" % (r + 1)
-        if r < 2:
-            quant(T[xq][:], T[xs][:], T[xn][:], [xn + str(b) for b in range(4)], [xq])
-            scores(r + 1)
-            send_state(r + 1)
-            quant(T.hq[:], T.hp[:], T.ht[:], ["ht%d" % b for b in range(4)], ["hq"])
-            mm(5, T.urq[:], T.urs[:], T.hq[:], T.hp[:], ["urq", "urs", "hq"])
+            cp("va"[b % 2], T.z[:, b:4 * C:4], T["t%d" % b][:].indirect(SN), ["t%d" % b] + snk, ["z%d" % b])
+            if b == 1:
+                for k in range(EARLY[r], 4):
+                    cp("av"[k % 2], T["w%d" % k][:], T["ps%d" % k][:, 0:C], ["ps%d" % k], ["w%d" % k])
+        parts = ((0, HALF), (HALF, C))
+
+        def lay(b, h):
+            lo, hi = parts[h]
+            cp("av"[b // 2], T.za[:, 4 * lo + b:4 * hi:4], T["w%d" % b][:].indirect(T[pl][:, lo // 16:hi // 16]), ["w%d" % b, pl], ["za%d%d" % (b, h)])
+
+        def answer(h):
+            lo, hi = parts[h]
+            quant(T.zq[:, lo:hi], T.zp[:, lo:hi], T.za[:, 4 * lo:4 * hi], ["za%d%d" % (b, h) for b in range(4)], ["zq%d" % h])
             for b in range(4):
-                unpack(b, xq, xs)
-            gk = "g%d" % (r + 1)
+                mm(4 * h + b, T.wq[:, 128 * b:128 * b + 128], T.wp[:, 128 * b:128 * b + 128], T.zq[:, lo:hi], T.zp[:, lo:hi], ["wq", "wp", "zq%d" % h], hi - lo)
+
+        def scale(q, b, h):
+            lo, hi = parts[h]
+            bank = "ps%d" % (4 * h + b)
+            scaled(q, T["h%d" % b][:, lo:hi], T[bank][:, 0:hi - lo], 0.03125, 0, [bank], ["h%d%d" % (b, h)])
+
+        for b in (0, 3, 1, 2):
+            lay(b, 0)
+        lay(0, 1)
+        lay(3, 1)
+        answer(0)
+        lay(1, 1)
+        lay(2, 1)
+        answer(1)
+        hl = pl
+        if not last:
+            pick(T.EN[:, 0:96], T.G0[:, 16 * 20:16 * NC], 96, keys("G0", 20, NC), ["EN"], 15)
+            ts(T[sn][:, 0:STAGES], T.EN[:, 15:96:16], CN, -1.0, A.mult, A.add, ["EN", "cp"], keys(sn, 0, STAGES))
+        else:
+            hl = "pn"
+            ts(T.qq[:], T[pl][:], -7.5, 1.0 / 16, A.add, A.mult, [pl], ["qq"])
+            ts(T.ra[:, 0:20], T[pl][:], 20.0, 19.0, A.mult, A.add, [pl], ["ra0"])
+            ts(T.ra[:, 20:40], T.qq[:], -321.0, None, A.mult, None, ["qq"], ["ra1"])
+            tt(T.ra[:, 40:60], T.ra[:, 0:20], T.ra[:, 20:40], A.add, ["ra0", "ra1"], ["ra2"])
+            cpv(T.pn[:], T.ra[:, 40:60], ["ra2"], ["pn"])
+        scale("a", 0, 0)
+        scale("a", 1, 0)
+        scale("a", 0, 1)
+        scale("a", 1, 1)
+        xq, xs = "xq%d" % (r + 1), "xs%d" % (r + 1)
+        for b in range(4):
+            if b >= 2:
+                scale("a", b, 0)
+                scale("a", b, 1)
+            if b == 0:
+                cpg(T.ht[:, 0:4 * C:4], T.h0[:], ["h00", "h01"], ["ht0"])
+            if b == 3:
+                for k in range(1, 4):
+                    cpa(T.ht[:, k:4 * C:4], T["h%d" % k][:], ["h%d0" % k, "h%d1" % k], ["ht%d" % k])
+                quant(T.hq[:], T.hp[:], T.ht[:], ["ht%d" % k for k in range(4)], ["hq"])
+                mm(5, T.urq[:], T.urs[:], T.hq[:], T.hp[:], ["urq", "urs", "hq"])
+            tt(T[xn][:, b:4 * C:4], T["h%d" % b][:].indirect(T[hl][:]), T.z[:, b:4 * C:4], A.add, ["h%d0" % b, "h%d1" % b, hl, "z%d" % b], [xn + str(b)])
+        if last:
+            break
+        gk = "g%d" % (r + 1)
+        ts(T[gk][:], T.ps5[:, 0:C], 0.0, None, A.is_gt, None, ["ps5"], [gk])
+        quant(T[xq][:], T[xs][:], T[xn][:], [xn + str(b) for b in range(4)], [xq])
+        scores(xq, xs)
+        send_state(r + 1)
+        for b in range(4):
+            unpack(b, xq, xs)
+        if r == 0:
+            plus(T.uu[:], T.g1[:], T.b0p[:], ["g1", "b0p"], ["uu"])
             ts(T.tt[:], T.ps4[:, 0:C], 0.0, float(L), A.is_gt, A.mult, ["ps4"], ["tt"])
-            ts(T[gk][:], T.ps5[:, 0:C], 0.0, None, A.is_gt, None, ["ps5"], [gk])
-            plus(T.uu[:], T.tt[:], T.b0[:], ["tt", "b0"], ["uu"])
-            if r == 1:
-                tt(T.x12[:], T.g1[:], T.g2[:], A.not_equal, ["g1", "g2"], ["x12"])
-                gk = "x12"
-            plus(T.pk[:], T[gk][:], T.uu[:], [gk, "uu"], ["pk"])
-    quant(T.hq[:], T.hp[:], T.ht[:], ["ht%d" % b for b in range(4)], ["hq"])
-    mm(5, T.urq[:], T.urs[:], T.hq[:], T.hp[:], ["urq", "urs", "hq"])
+            cpa(T.W4[:, 0:320], IDN.indirect(T.lab[:, 0:20]), ["idn", "lab"], ["W4a"])
+            cpa(T.W4[:, 320:640], IDN.indirect(T.lab[:, 20:40]), ["idn", "lab"], ["W4b"])
+            scaled("a", T.X16[:], POS, 1 / UP, 0, ["pos"], ["X16"])
+        else:
+            tt(T.x12[:], T.g1[:], T.g2[:], A.not_equal, ["g1", "g2"], ["x12"])
+            ts(T.tt[:], T.ps4[:, 0:C], 0.0, float(L), A.is_gt, A.mult, ["ps4"], ["tt"])
+            plus(T.uu[:], T.x12[:], T.b0p[:], ["x12", "b0p"], ["uu"])
+            scaled("a", T.X16[:], T.x12[:].indirect(T.rho[:]), 1 / UP, 0, ["x12", "rho"], ["X16"])
+            cpg(T.W4[:, 640:1280], T.W4[:, 0:640], ["W4a", "W4b"], ["W4c"], 640)
+        plus(T.pk[:], T.tt[:], T.uu[:], ["tt", "uu"], ["pk"])
+    cpa(T.ob[:, 0:320], T.nat[:].indirect(SN), ["nat"] + snk, ["obs"])
+    store("ops", T.op[:, 0:320], T.ob[0:128:16, 0:320], ["obs"])
+    ts(T.NR[:], T.ps5[:, 0:C], 0.0, C / UP, A.is_gt, A.mult, ["ps5"], ["NRa", "NRb"])
     quant(T.xq3[:], T.xs3[:], T.xn2[:], ["xn2%d" % b for b in range(4)], ["xq3"])
     mm(6, T.vq[:], T.vs[:], T.xq3[:], T.xs3[:], ["vq", "xq3"])
     store("oc", T.oc[:, :], T.xq3[:, :].bitcast(dt.uint8), ["xq3"])
@@ -350,13 +447,12 @@ def rank_program(g, core, T, topo):
         store("os%d" % k, T.osc[4 * k:4 * k + 4, :], T.xs3[32 * k:32 * k + 4, :], ["xq3"])
     cpa(T.yb[:], T.ps6[:, 0:C], ["ps6"], ["yb"])
     store("y", T.y[:, :], T.yb[:], ["yb"])
-    ts(T.g3[:], T.ps5[:, 0:C], 0.0, 320.0, A.is_gt, A.mult, ["ps5"], ["g3"])
-    plus(T.fin[:], T.g3[:], T.b4s[:], ["g3", "b4s"], ["fin"])
-    scan(T.tt[:], T.M0[:], T.fin[:], 0.0, A.mult, A.add, ["fin", "M0"], ["tt"])
-    ts(T.lfa[:], T.tt[:, 15:320:16], CQ, -float(BIG), A.mult, A.add, ["tt", "cq"], ["lfa"])
-    ts(T.lfb[:], T.tt[:, 15:320:16], CQ, 320.0 - BIG, A.mult, A.add, ["tt", "cq"], ["lfb"])
-    w4 = ["W4a", "W4b", "W4c", "W4d"]
-    op("a", lambda: S.activation(T.ob[:, 320:640], T.W4[:, :].indirect(T.lfa[:]), ACT.Identity, bias=-1.0, scale=UP), w4 + ["lfa"], ["oba"])
-    ts(T.ob[:, 640:960], T.W4[:, :].indirect(T.lfb[:]), UP, -1.0, A.mult, A.add, w4 + ["lfb"], ["obb"])
+    pick(T.EN[:], T.NR[:], C, ["NRa", "NRb"], ["EN"])
+    tt(T.rr[:, 0:20], T.EN[:, 15:C:16], T.bl[:, 40:60], A.add, ["EN", "bl2"], ["r0"])
+    ts(T.lfa[:], T.rr[:, 0:20], CP, None, A.mult, None, ["r0", "cp"], ["lfa"])
+    ts(T.lfb[:], T.rr[:, 0:20], CP, float(C), A.mult, A.add, ["r0", "cp"], ["lfb"])
+    w4 = ["W4a", "W4b", "W4c"]
+    scaled("v", T.ob[:, 320:640], T.W4[:, :].indirect(T.lfa[:]), 1, -1, w4 + ["lfa"], ["oba"])
+    scaled("a", T.ob[:, 640:960], T.W4[:, :].indirect(T.lfb[:]), 1, -1, w4 + ["lfb"], ["obb"])
     store("opt", T.op[:, 320:960], T.ob[0:128:16, 320:960], ["oba", "obb"])
     learn("g", [(s, n) for s, n in count.items()])

@@ -3,16 +3,21 @@ from concourse.mybir import dt, AluOpType, ActivationFunctionType
 STEP = [1, 2, 4]
 C, STAGES = 320, 6
 L = 1536
-BIG = 4096
+U = 2.0 ** -12
+LOW = 1 - L * U
+HT = 160
 UP = 2.0 ** 24
 MID = 480
 WIN = L + 3 * C
 NC = 20 + STAGES
-CHAINS = [(0, 14), (14, 26)]
+CHAINS = [(0, 16), (16, 26)]
 SHARE = [0, 0]
-EARLY = [1, 2, 2]
+OWN = [0, 2, 2]
+EARLY = [1, 4, 1]
 FIRST = 12
-HALF = 192
+HALF = 16 * (CHAINS[0][1] - STAGES)
+BEFORE = [("v", 2, 0), ("a", 3, 0), ("v", 0, 1), ("a", 1, 1), ("a", 3, 1)]
+AFTER = [("v", 2, 1)]
 SCRATCH = {}
 
 
@@ -23,24 +28,28 @@ def _declare(names, where, cols, dtype):
 
 F8, U8 = "float8_e4m3fn_x4", "uint8"
 _declare("sti qq e16", "sbuf", 20, "int32")
-_declare("tab tq", "sbuf", 40, "int32")
+_declare("tab tq", "sbuf", 60, "int32")
 _declare("lci lq", "sbuf", NC, "int32")
 _declare("kp kk", "sbuf", NC + 2, "int32")
 _declare("d16 dd", "sbuf", 16, "int32")
 _declare("lui", "sbuf", 8, "int32")
 _declare("lu", "sbuf", 8, "uint16")
 _declare("lk", "sbuf", NC + 2, "uint16")
-_declare("rho ls lfa lfb pl0 pl1 pl2 pn", "sbuf", 20, "uint16")
-_declare("lab lpos", "sbuf", 40, "uint16")
+_declare("ls lfa lfb pl0 pl1 pl2 pn", "sbuf", 20, "uint16")
+_declare("lab", "sbuf", 40, "uint16")
+_declare("lpos", "sbuf", 60, "uint16")
 _declare("lc o0 o1 sc sn0 sn1 sn2", "sbuf", NC, "uint16")
 _declare("rr pp bl ra", "sbuf", 64, "float32")
-_declare("rt", "sbuf", 120, "float32")
+_declare("rt", "sbuf", 180, "float32")
 _declare("sm", "sbuf", 8, "float32")
 _declare("M", "sbuf", 16 * (NC + 2), "bfloat16")
 _declare("G0 G1", "sbuf", 16 * NC, "float16")
 _declare("E0 E1", "sbuf", 16 * (NC + len(CHAINS)), "float16")
 _declare("NR EN X16", "sbuf", C, "float16")
-_declare("G6 nat b0 b0p uu g1 g2 x12 fin tt pk yb", "sbuf", C, "float32")
+_declare("b0 b0p", "sbuf", C, "float16")
+_declare("D0 D1 D2", "sbuf", 2 * C, "float16")
+_declare("G6 nat fin pk yb", "sbuf", C, "float32")
+_declare("g1 sg x12 tt", "sbuf", C, "bfloat16")
 _declare("W W6", "sbuf", WIN, "float32")
 _declare("W4", "sbuf", 1280, "float32")
 _declare("ob", "sbuf", 960, "float32")
@@ -55,8 +64,8 @@ for _q, _p, _n in (("wq", "wp", 512), ("uq", "us", 128), ("urq", "urs", 128), ("
 _declare("rq0 rq1 rq2 xq0 xq1 xq2 xq3", "sbuf", C, F8)
 _declare("rp0 rp1 rp2 xs0 xs1 xs2 xs3", "sbuf", C, U8)
 _declare("ps0 ps1 ps2 ps3 ps4 ps5 ps6 ps7", "psum", 512, "float32")
-SEMAPHORES = ("cv ct ca cg sent gotl0 gotl1 gotl2 gotz0 gotz1 gotz2 ld_st ld_x ld_ta ld_tb ld_u ld_wc ld_ws ld_v "
-              "sv_y sv_ops sv_opt sv_oc sv_os0 sv_os1 sv_os2 sv_os3").split()
+SEMAPHORES = ("cv ct ca cg sent gotl00 gotl01 gotl10 gotl11 gotl20 gotz0 gotz1 gotz2 ld_st ld_x ld_ta ld_tb ld_u ld_wc ld_ws ld_v "
+              "sv_y0 sv_y1 sv_ops sv_opt sv_oc0 sv_oc1 sv_os0 sv_os1 sv_os2 sv_os3").split()
 
 
 def rank_program(g, core, T, topo):
@@ -152,7 +161,7 @@ def rank_program(g, core, T, topo):
         scan(out, T.M[:, first:first + n], row, 0.0, A.mult, A.add, rd + ["M"], wr)
 
     def plus(out, a, b, rd, wr):
-        scan(out, a, b, float(BIG), A.min, A.add, rd, wr)
+        scan(out, a, b, 1.0, A.min, A.add, rd, wr)
 
     def quant(codes, plane, tile, rd, wr):
         op("v", lambda: V.quantize_mx(codes, plane, tile), rd, wr)
@@ -188,6 +197,7 @@ def rank_program(g, core, T, topo):
     iota(T.W[:, 3 * C:L], [[1, L - 3 * C]], 1, 0, "idn", True)
     op("g", lambda: g.affine_select(T.et[:, 3:515:4], T.one[:], [[-1, 128]], A.is_equal, 0.0, 0, 1), ["one"], ["et"])
     iota(T.W6[:, 3 * C:L + 4], [[1, 29], [-16, 20]], 304 + 1, 0, "pos", True)
+    iota(T.e16[:], [[16, 20]], 0, 0, "e16")
     ts(T.dd[:], T.d16[:], 15, None, A.bitwise_and, None, ["d16"], ["dd"])
     ts(T.kk[:], T.kp[:], 15, None, A.bitwise_and, None, ["kp"], ["kk"])
     ts(T.pp[:, 0:16], T.dd[:], 1, UP, A.is_equal, A.mult, ["dd"], ["p0"])
@@ -207,7 +217,7 @@ def rank_program(g, core, T, topo):
     cpv(T.lc[:], T.rr[:, 32:32 + NC], ["r1"], ["lc"])
     scaled("a", T.fin[:], IDN.indirect(T.ls[:]), 1 / UP, 0, ["idn", "ls"], ["fin"])
     quant(T.uq[:], T.us[:], T.ui[:], ["ui"], ["uq"])
-    cpv(T.lab[:], T.tab[:], ["ta", "tb"], ["lab"])
+    cpv(T.lab[:], T.tab[:, 0:40], ["ta", "tb"], ["lab"])
     cpv(T.urq[:, 0:128].bitcast(dt.uint32), T.uq[:, 0:128].bitcast(dt.uint32).indirect(T.lu[:, 0:8]), ["uq", "lu"], ["urq"])
     cpa(T.urs[:, 0:128], T.us[:, 0:128].indirect(T.lu[:, 0:8]), ["uq", "lu"], ["urs"])
     cpa(T.G1[:, :], T.fin[:].indirect(T.lc[:, :]), ["fin", "lc"], keys("G1", 0, NC))
@@ -215,11 +225,19 @@ def rank_program(g, core, T, topo):
     def scores(q, p):
         mm(4, T.urq[:], T.urs[:], T[q][:], T[p][:], ["urq", "urs", q])
 
+    def signs(h):
+        ts(T.tt[:, 160 * h:160 * h + 160], T["ps%d" % (6 + h)][:, 0:160], 0.0, LOW, A.is_gt, A.max, ["ps%d" % (6 + h)], ["tt%d" % h])
+
     def unpack(b, q, p):
         mm(b, T.eq[:, 128 * b:128 * b + 128], T.es[:, 128 * b:128 * b + 128], T[q][:], T[p][:], ["eq%d" % b, q, p])
 
+    def own(b, r):
+        cpa(T["t%d" % b][:], T["ps%d" % b][:, 0:C], ["ps%d" % b], ["t%d" % b])
+        unpack(b, "rq%d" % r, "rp%d" % r)
+
     def unit(b):
         quant(T.eq[:, 128 * b:128 * b + 128], T.es[:, 128 * b:128 * b + 128], T.et[:, 3 - b:515 - b], ["et"], ["eq%d" % b])
+        unpack(b, "xq0", "xs0")
 
     def partner(r):
         other = T.cores[rank ^ STEP[r]]
@@ -234,22 +252,16 @@ def rank_program(g, core, T, topo):
         count["sent"] = count.get("sent", 0) + 2 * ne
         wrote[rq] = [(sem, 2 * ne)]
 
-    scaled("v", T.b0[:], IDN, 3, BIG - 3, ["idn"], ["b0"])
-    unit(0)
-    unit(1)
+    scaled("v", T.b0[:], IDN, 3 * U, -2 * U, ["idn"], ["b0"])
     quant(T.iq[:], T.ip[:], T.xi[:], ["xi"], ["iq"])
     scores("iq", "ip")
-    pick(T.E1[:, 0:16 * NC], T.G1[:, :], 16 * NC, keys("G1", 0, NC), keys("E1", 0, NC))
     cpv(T.xq0[:, :].bitcast(dt.uint32), T.iq[:, :].bitcast(dt.uint32).indirect(T.lc[:, STAGES:NC]), ["iq", "lc"], ["xq0"])
     cpa(T.xs0[:, :], T.ip[:, :].indirect(T.lc[:, STAGES:NC]), ["iq", "lc"], ["xs0"])
     send_state(0)
-    ts(T.tt[:], T.ps4[:, 0:C], 0.0, float(L), A.is_gt, A.mult, ["ps4"], ["tt"])
+    ts(T.tt[:], T.ps4[:, 0:C], 0.0, LOW, A.is_gt, A.max, ["ps4"], ["tt0", "tt1"])
+    pick(T.E1[:, 0:16 * NC], T.G1[:, :], 16 * NC, keys("G1", 0, NC), keys("E1", 0, NC))
+    plus(T.pk[:], T.b0[:], T.tt[:], ["tt0", "tt1", "b0"], ["pk0", "pk1"])
     ts(T.sc[:, :], T.E1[:, 15:16 * NC:16], CP, -1.0, A.mult, A.add, keys("E1", 0, NC) + ["cp"], keys("sc", 0, NC))
-    unit(2)
-    plus(T.pk[:], T.tt[:], T.b0[:], ["tt", "b0"], ["pk"])
-    unit(3)
-    for b in range(4):
-        unpack(b, "xq0", "xs0")
     scaled("a", slot("W6", 0), POS.indirect(T.lab[:, 0:20]), 1 / UP, 0, ["pos", "lab"], ["W60"])
     W6K = ["W60", "W61a", "W61b", "W62", "pos", "W63", "W64", "W65"]
     WK = ["W0", "W1", "W2", "W3", "W4", "W5", "idn"]
@@ -258,13 +270,13 @@ def rank_program(g, core, T, topo):
         rid, pid, mask, ne = partner(r)
         rq, rp, sn, pl, xn = [n + str(r) for n in ("rq", "rp", "sn", "pl", "xn")]
         lab, sc = ("lab", "sc") if r == 0 else ("lpos", "sn%d" % (r - 1))
-        small = (1 / UP, -(BIG + MID) / UP)
+        small = (1 / U / UP, -(LOW / U + 1 + MID) / UP)
         last = r == 2
 
         def gather(n, lo, hi, q):
             G, o = "G%d" % (n % 2), "o%d" % ((n + 1) % 2)
             if n == 0:
-                scaled(q, T.G0[:, 16 * lo:16 * hi], T.pk[:].indirect(T[sc][:, lo:hi]), small[0], small[1], ["pk"] + keys(sc, lo, hi), keys(G, lo, hi))
+                scaled(q, T.G0[:, 16 * lo:16 * hi], T.pk[:].indirect(T[sc][:, lo:hi]), small[0], small[1], ["pk0", "pk1"] + keys(sc, lo, hi), keys(G, lo, hi))
             elif n == STAGES and last:
                 cp(q, T.G6[:, 16 * (lo - n):16 * (hi - n)], T.W6[:, 0:WIN].indirect(T[o][:, lo:hi]), W6K + keys(o, lo, hi), keys("G6", lo, hi))
             else:
@@ -280,8 +292,8 @@ def rank_program(g, core, T, topo):
             o, more = ("o%d" % (n % 2), MID) if n < STAGES else (sn, -1)
             ts(T[o][:, lo:hi], T[E][:, 16 * (lo + i) + 15:16 * (hi + i):16], CP, float(more), A.mult, A.add, keys(E, lo + i, hi + i) + ["cp"], keys(o, lo, hi))
 
-        scaled("a", slot("W", 0), T.pk[:].indirect(T[lab][:, 0:20]), small[0], small[1], ["pk", lab], ["W0"])
-        scaled("v", slot("W", 1), T.pk[:].indirect(T[lab][:, 20:40]), small[0], small[1], ["pk", lab], ["W1"])
+        scaled("a", slot("W", 0), T.pk[:].indirect(T[lab][:, 0:20]), small[0], small[1], ["pk0", "pk1", lab], ["W0"])
+        scaled("v", slot("W", 1), T.pk[:].indirect(T[lab][:, 20:40]), small[0], small[1], ["pk0", "pk1", lab], ["W1"])
         gather(0, 0, FIRST, "v")
         gather(0, FIRST, NC, "a")
         cpg(slot("W", 3), slot("W", 0), ["W0"], ["W3"])
@@ -289,6 +301,8 @@ def rank_program(g, core, T, topo):
         cpv(slot("W", 4), slot("W", 1), ["W1"], ["W4"])
         cpa(slot("W", 5), slot("W", 0), ["W0"], ["W5"])
         row(0, 0, NC, 0)
+        if r == 0:
+            unit(0)
         cast(0, 0, NC, 0)
         gaps, fill = [], []
         if r == 0:
@@ -299,31 +313,47 @@ def rank_program(g, core, T, topo):
             def rest():
                 scaled("a", slot("W6", 1, 160, C), POS.indirect(T.lab[:, 30:40]), 1 / UP, 0, ["pos", "lab"], ["W61b"])
                 cpg(slot("W6", 4), slot("W6", 1), ["W61a", "W61b", "pos"], ["W64"])
-                iota(T.b0p[:], [[-3, 20], [60, 16]], 57 + BIG, 0, "b0p", True)
+                iota(T.nat[:], [[-1, 20], [20, 16]], 19, 0, "nat", True)
             gaps.append(rest)
-            fill += [lambda: ts(T.tq[:], T.tab[:], -9.5, 0.05, A.add, A.mult, ["ta", "tb"], ["tq"]),
-                     lambda: ts(T.rt[:, 0:40], T.tab[:], -16.0, 304.0, A.mult, A.add, ["ta", "tb"], ["rt0"]),
-                     lambda: ts(T.rt[:, 40:80], T.tq[:], 321.0, None, A.mult, None, ["tq"], ["rt1"]),
-                     lambda: tt(T.rt[:, 80:120], T.rt[:, 0:40], T.rt[:, 40:80], A.add, ["rt0", "rt1"], ["rt2"]),
-                     lambda: cpv(T.lpos[:], T.rt[:, 80:120], ["rt2"], ["lpos"])]
+            tab = ["ta", "tb", "tc"]
+            fill += [(lambda b=b: unit(b)) for b in range(1, 4)]
+            fill += [lambda: tt(T.tab[:, 40:60], T.e16[:], T.kk[:, 0:20], A.add, ["e16", "kk"], ["tc"]),
+                     lambda: ts(T.tq[:], T.tab[:], -9.5, 0.05, A.add, A.mult, tab, ["tq"]),
+                     lambda: ts(T.rt[:, 0:60], T.tab[:], -16.0, 304.0, A.mult, A.add, tab, ["rt0"]),
+                     lambda: ts(T.rt[:, 60:120], T.tq[:], 321.0, None, A.mult, None, ["tq"], ["rt1"]),
+                     lambda: tt(T.rt[:, 120:180], T.rt[:, 0:60], T.rt[:, 60:120], A.add, ["rt0", "rt1"], ["rt2"]),
+                     lambda: cpv(T.lpos[:], T.rt[:, 120:180], ["rt2"], ["lpos"])]
         if r == 1:
-            fill += [lambda: pick(T.NR[:], T.X16[:], C, ["X16"], ["NRa", "NRb"]),
-                     lambda: ts(T.rho[:], T.NR[:, 15:C:16], CP, -1.0, A.mult, A.add, ["NRa", "NRb", "cp"], ["rho"]),
+            fill += [lambda: op("v", lambda: V.memset(T.D0[:, 0:2 * C:2], 0.0), [], ["D0e"]),
+                     lambda: ts(T.D0[:, 1:2 * C:2], T.g1[:], -2.0, U, A.mult, A.add, ["g0", "g1"], ["D0o"]),
                      lambda: quant(T.vq[:], T.vs[:], T.vi[:], ["vi"], ["vq"]),
-                     lambda: tt(T.qq[:], T.e16[:], T.kk[:, 0:20], A.add, ["e16", "kk"], ["qq"]),
-                     lambda: ts(T.bl[:, 0:20], T.qq[:], CQ, None, A.mult, None, ["qq", "cq"], ["bl0"])]
+                     lambda: ts(T.bl[:, 0:20], T.tab[:, 40:60], CQ, None, A.mult, None, ["tc", "cq"], ["bl0"])]
         if last:
+            fill += [lambda: scan(T.x12[:], T.D2[:, 1:2 * C:2], T.b0p[:], 0.0, A.max, A.subtract, ["uu0", "uu1", "b0p"], ["x12"])]
+            fill += [None] * 5
             fill += [lambda: pick(T.EN[:], T.X16[:], C, ["X16"], ["EN"]),
                      lambda: ts(T.bl[:, 20:40], T.EN[:, 15:C:16], CP, 0.5, A.mult, A.is_gt, ["EN", "cp"], ["bl1"]),
                      lambda: ts(T.bl[:, 20:40], T.bl[:, 20:40], CQ, float(C), A.mult, A.mult, ["bl1", "cq"], ["bl1"]),
                      lambda: tt(T.bl[:, 40:60], T.bl[:, 20:40], T.bl[:, 0:20], A.add, ["bl0", "bl1"], ["bl2"])]
 
-        def own(b):
-            cpa(T["t%d" % b][:], T["ps%d" % b][:, 0:C], ["ps%d" % b], ["t%d" % b])
-            unpack(b, rq, rp)
-        gaps += [(lambda b=b: own(b)) for b in range(4)]
+        gaps += [(lambda b=b: own(b, r)) for b in range(OWN[r], 4)]
+        if last:
+            gaps[1:1] = [lambda h=h: scaled("a", T.X16[:, 160 * h:160 * h + 160], T.x12[:].indirect(T.lpos[:, 40 + 10 * h:50 + 10 * h]),
+                                            1 / U / UP, 0, ["x12", "lpos"], ["X16"]) for h in range(2)]
         gaps += [(lambda b=b: cpa(T["w%d" % b][:], T["ps%d" % b][:, 0:C], ["ps%d" % b], ["w%d" % b])) for b in range(EARLY[r])]
         steps = [(n, i) for n in range(1, STAGES + 1) for i in range(2)]
+        parts = ((0, HALF), (HALF, C))
+
+        def send_list(lo, hi, i):
+            learn("g", [tok for k in keys(sn, lo, hi) for tok in wrote[k]])
+            g.remote_dma(T[pl][:, lo - STAGES:hi - STAGES], T[sn][:, lo:hi], T.sem["gotl%d%d" % (r, i)], T.sem.sent, pid, rid, mask)
+            count["sent"] += ne
+            wrote[pl + str(i)] = [("gotl%d%d" % (r, i), ne)]
+
+        def mosaic(q, b, h):
+            lo, hi = parts[h]
+            a, e = STAGES + lo // 16, STAGES + hi // 16
+            cp(q, T.z[:, 4 * lo + b:4 * hi:4], T["t%d" % b][:].indirect(T[sn][:, a:e]), ["t%d" % b] + keys(sn, a, e), ["z%d%d" % (b, h)])
 
         def span(n, i):
             return (max(CHAINS[i][0], n - n % 2), CHAINS[i][1])
@@ -333,6 +363,9 @@ def rank_program(g, core, T, topo):
             behind = t > 0 and not (last and n == STAGES)
             if behind:
                 row(n, span(n, i)[0] - (i if n < STAGES else 0), span(n, i)[1], i)
+            if t == len(steps) and not last:
+                mosaic("v", 0, 0)
+                mosaic("a", 1, 0)
             if t < len(steps):
                 lo, hi = span(*steps[t])
                 cut = (lo + hi) // 4 * 2 + SHARE[steps[t][1]]
@@ -342,62 +375,69 @@ def rank_program(g, core, T, topo):
                     gaps.pop(0)()
             if behind:
                 cast(n, span(min(n + 1, STAGES), i)[0], span(n, i)[1], i)
-            if t > 1 and fill:
-                fill.pop(0)()
+                if n == STAGES:
+                    send_list(span(n, i)[0], span(n, i)[1], i)
+            if (t > 1 or r == 0) and fill:
+                (fill.pop(0) or list)()
+            if t == len(steps) and not last:
+                break
         if last:
-            cpv(T.NR[:, 0:160], T.G6[:, :].indirect(T.rho[:, 0:10]), keys("G6", STAGES, NC) + ["rho"], ["NRa"])
-            cpa(T.NR[:, 160:320], T.G6[:, :].indirect(T.rho[:, 10:20]), keys("G6", STAGES, NC) + ["rho"], ["NRb"])
+            cpv(T.NR[:, 0:160], T.G6[:, :].indirect(T.lpos[:, 40:50]), keys("G6", STAGES, NC) + ["lpos"], ["NRa"])
+            cpa(T.NR[:, 160:320], T.G6[:, :].indirect(T.lpos[:, 50:60]), keys("G6", STAGES, NC) + ["lpos"], ["NRb"])
             pick(T.EN[:], T.NR[:], C, ["NRa", "NRb"], ["EN"])
             ts(T[sn][:, STAGES:NC], T.EN[:, 15:C:16], CP, -1.0, A.mult, A.add, ["EN", "cp"], keys(sn, STAGES, NC))
         snk, SN = keys(sn, STAGES, NC), T[sn][:, STAGES:NC]
-        learn("g", [tok for k in snk for tok in wrote[k]])
-        g.remote_dma(T[pl][:, :], SN, T.sem["gotl%d" % r], T.sem.sent, pid, rid, mask)
-        count["sent"] += ne
-        wrote[pl] = [("gotl%d" % r, ne)]
-        if r == 0:
-            iota(T.nat[:], [[-1, 20], [20, 16]], 19, 0, "nat", True)
-            iota(T.e16[:], [[16, 20]], 0, 0, "e16")
-        for b in range(4):
-            cp("va"[b % 2], T.z[:, b:4 * C:4], T["t%d" % b][:].indirect(SN), ["t%d" % b] + snk, ["z%d" % b])
-            if b == 1:
-                for k in range(EARLY[r], 4):
-                    cp("av"[k % 2], T["w%d" % k][:], T["ps%d" % k][:, 0:C], ["ps%d" % k], ["w%d" % k])
-        parts = ((0, HALF), (HALF, C))
+        if last:
+            send_list(STAGES, NC, 0)
+            wrote[pl + "1"] = wrote[pl + "0"]
+            mosaic("v", 0, 0)
+            mosaic("a", 1, 0)
+        for k in range(EARLY[r], 4):
+            cp("av"[k % 2], T["w%d" % k][:], T["ps%d" % k][:, 0:C], ["ps%d" % k], ["w%d" % k])
+        for q, b, h in BEFORE:
+            mosaic(q, b, h)
 
         def lay(b, h):
             lo, hi = parts[h]
-            cp("av"[b // 2], T.za[:, 4 * lo + b:4 * hi:4], T["w%d" % b][:].indirect(T[pl][:, lo // 16:hi // 16]), ["w%d" % b, pl], ["za%d%d" % (b, h)])
+            cp("av"[b // 2], T.za[:, 4 * lo + b:4 * hi:4], T["w%d" % b][:].indirect(T[pl][:, lo // 16:hi // 16]), ["w%d" % b, pl + str(h)], ["za%d%d" % (b, h)])
 
         def answer(h):
             lo, hi = parts[h]
             quant(T.zq[:, lo:hi], T.zp[:, lo:hi], T.za[:, 4 * lo:4 * hi], ["za%d%d" % (b, h) for b in range(4)], ["zq%d" % h])
-            for b in range(4):
-                mm(4 * h + b, T.wq[:, 128 * b:128 * b + 128], T.wp[:, 128 * b:128 * b + 128], T.zq[:, lo:hi], T.zp[:, lo:hi], ["wq", "wp", "zq%d" % h], hi - lo)
+            for b in range(4 if h else 2):
+                lo, hi = parts[h] if b < 2 else (0, C)
+                mm(b + (4 * h if b < 2 else 0), T.wq[:, 128 * b:128 * b + 128], T.wp[:, 128 * b:128 * b + 128], T.zq[:, lo:hi], T.zp[:, lo:hi],
+                   ["wq", "wp", "zq0", "zq%d" % h], hi - lo)
 
         def scale(q, b, h):
-            lo, hi = parts[h]
+            lo, hi = parts[h] if b < 2 else (0, C)
             bank = "ps%d" % (4 * h + b)
             scaled(q, T["h%d" % b][:, lo:hi], T[bank][:, 0:hi - lo], 0.03125, 0, [bank], ["h%d%d" % (b, h)])
 
-        for b in (0, 3, 1, 2):
+        for b in (0, 2, 1, 3):
             lay(b, 0)
+        if last:
+            ts(T.qq[:], T[pl][:], -7.5, 1.0 / 16, A.add, A.mult, [pl + "0"], ["qq"])
         lay(0, 1)
-        lay(3, 1)
+        lay(2, 1)
         answer(0)
         lay(1, 1)
-        lay(2, 1)
+        lay(3, 1)
+        if last:
+            ts(T.ra[:, 0:20], T[pl][:], 20.0, 19.0, A.mult, A.add, [pl + "0"], ["ra0"])
+            ts(T.ra[:, 20:40], T.qq[:], -321.0, None, A.mult, None, ["qq"], ["ra1"])
         answer(1)
-        hl = pl
+        hl = "pn" if last else pl
         if not last:
             pick(T.EN[:, 0:96], T.G0[:, 16 * 20:16 * NC], 96, keys("G0", 20, NC), ["EN"], 15)
+            mosaic(*AFTER[0])
             ts(T[sn][:, 0:STAGES], T.EN[:, 15:96:16], CN, -1.0, A.mult, A.add, ["EN", "cp"], keys(sn, 0, STAGES))
         else:
-            hl = "pn"
-            ts(T.qq[:], T[pl][:], -7.5, 1.0 / 16, A.add, A.mult, [pl], ["qq"])
-            ts(T.ra[:, 0:20], T[pl][:], 20.0, 19.0, A.mult, A.add, [pl], ["ra0"])
-            ts(T.ra[:, 20:40], T.qq[:], -321.0, None, A.mult, None, ["qq"], ["ra1"])
             tt(T.ra[:, 40:60], T.ra[:, 0:20], T.ra[:, 20:40], A.add, ["ra0", "ra1"], ["ra2"])
+            mosaic(*AFTER[0])
             cpv(T.pn[:], T.ra[:, 40:60], ["ra2"], ["pn"])
+        for q, b, h in AFTER[1:]:
+            mosaic(q, b, h)
         scale("a", 0, 0)
         scale("a", 1, 0)
         scale("a", 0, 1)
@@ -406,53 +446,74 @@ def rank_program(g, core, T, topo):
         for b in range(4):
             if b >= 2:
                 scale("a", b, 0)
-                scale("a", b, 1)
             if b == 0:
                 cpg(T.ht[:, 0:4 * C:4], T.h0[:], ["h00", "h01"], ["ht0"])
+                cpg(T.ht[:, 1:4 * HT:4], T.h1[:, 0:HT], ["h10", "h11"], ["ht4"], HT)
             if b == 3:
-                for k in range(1, 4):
-                    cpa(T.ht[:, k:4 * C:4], T["h%d" % k][:], ["h%d0" % k, "h%d1" % k], ["ht%d" % k])
-                quant(T.hq[:], T.hp[:], T.ht[:], ["ht%d" % k for k in range(4)], ["hq"])
+                cpa(T.ht[:, 4 * HT + 1:4 * C:4], T.h1[:, HT:C], ["h10", "h11"], ["ht1"])
+                for k in range(2, 4):
+                    cpa(T.ht[:, k:4 * C:4], T["h%d" % k][:], ["h%d0" % k], ["ht%d" % k])
+                quant(T.hq[:], T.hp[:], T.ht[:], ["ht%d" % k for k in range(5)], ["hq"])
                 mm(5, T.urq[:], T.urs[:], T.hq[:], T.hp[:], ["urq", "urs", "hq"])
-            tt(T[xn][:, b:4 * C:4], T["h%d" % b][:].indirect(T[hl][:]), T.z[:, b:4 * C:4], A.add, ["h%d0" % b, "h%d1" % b, hl, "z%d" % b], [xn + str(b)])
+                if r == 0:
+                    scaled("a", T.b0p[:], T.nat[:], 3 * U, U, ["nat"], ["b0p"])
+                    cpa(T.W4[:, 0:320], IDN.indirect(T.lab[:, 0:20]), ["idn", "lab"], ["W4a"])
+                if r == 1:
+                    cpa(T.W4[:, 320:640], IDN.indirect(T.lab[:, 20:40]), ["idn", "lab"], ["W4b"])
+            for lo, hi, hs in ([(0, C, "01")] if b < 3 else [(0, 160, "0"), (160, C, "1")]):
+                tt(T[xn][:, 4 * lo + b:4 * hi:4], T["h%d" % b][:].indirect(T[hl][:, lo // 16:hi // 16]), T.z[:, 4 * lo + b:4 * hi:4], A.add,
+                   ["h%d0" % b, "h%d1" % b, hl, pl + "0", pl + "1", "z%d0" % b, "z%d1" % b], [xn + str(b) + h for h in hs])
         if last:
             break
-        gk = "g%d" % (r + 1)
-        ts(T[gk][:], T.ps5[:, 0:C], 0.0, None, A.is_gt, None, ["ps5"], [gk])
-        quant(T[xq][:], T[xs][:], T[xn][:], [xn + str(b) for b in range(4)], [xq])
-        scores(xq, xs)
+        for h in range(2):
+            lo, hi = 160 * h, 160 * h + 160
+            quant(T[xq][:, lo:hi], T[xs][:, lo:hi], T[xn][:, 4 * lo:4 * hi], [xn + str(b) + str(h) for b in range(4)], [xq + "h%d" % h])
+            mm(6 + h, T.urq[:], T.urs[:], T[xq][:, lo:hi], T[xs][:, lo:hi], ["urq", "urs", xq + "h%d" % h], 160)
+        wrote[xq] = wrote[xq + "h1"]
         send_state(r + 1)
         for b in range(4):
             unpack(b, xq, xs)
-        if r == 0:
-            plus(T.uu[:], T.g1[:], T.b0p[:], ["g1", "b0p"], ["uu"])
-            ts(T.tt[:], T.ps4[:, 0:C], 0.0, float(L), A.is_gt, A.mult, ["ps4"], ["tt"])
-            cpa(T.W4[:, 0:320], IDN.indirect(T.lab[:, 0:20]), ["idn", "lab"], ["W4a"])
-            cpa(T.W4[:, 320:640], IDN.indirect(T.lab[:, 20:40]), ["idn", "lab"], ["W4b"])
-            scaled("a", T.X16[:], POS, 1 / UP, 0, ["pos"], ["X16"])
-        else:
-            tt(T.x12[:], T.g1[:], T.g2[:], A.not_equal, ["g1", "g2"], ["x12"])
-            ts(T.tt[:], T.ps4[:, 0:C], 0.0, float(L), A.is_gt, A.mult, ["ps4"], ["tt"])
-            plus(T.uu[:], T.x12[:], T.b0p[:], ["x12", "b0p"], ["uu"])
-            scaled("a", T.X16[:], T.x12[:].indirect(T.rho[:]), 1 / UP, 0, ["x12", "rho"], ["X16"])
+        D = T.D1 if r == 0 else T.D2
+        for h in range(2):
+            lo, hi = 160 * h, 160 * h + 160
+            op("a", lambda: S.activation(T.sg[:, lo:hi], T.ps5[:, lo:hi], ACT.Sign), ["ps5"], ["sg%d" % h])
+        for h in range(2):
+            lo, hi = 160 * h, 160 * h + 160
+            out, scl = (T.g1[:, lo:hi], U) if r == 0 else (T.D1[:, 2 * lo:2 * hi:2], 1.0)
+            op("a", lambda: S.activation(out, T.sg[:, lo:hi], ACT.Relu, scale=scl), ["sg%d" % h], ["g%d" % h if r == 0 else "D1e%d" % h])
+        for h in range(2):
+            lo, hi = 160 * h, 160 * h + 160
+            signs(h)
+            if r == 0:
+                plus(T.D1[:, 2 * lo + 1:2 * hi:2], T.g1[:, lo:hi], T.b0p[:, lo:hi], ["g%d" % h, "b0p"], ["uu%d" % h])
+            else:
+                scan(T.D2[:, 2 * lo:2 * hi], T.D0[:, 2 * lo:2 * hi], T.D1[:, 2 * lo:2 * hi], 0.0, A.mult, A.add, ["D0e", "D0o", "D1e%d" % h], ["uu%d" % h])
+        for b in range(OWN[r + 1]):
+            own(b, r + 1)
+        if r == 1:
             cpg(T.W4[:, 640:1280], T.W4[:, 0:640], ["W4a", "W4b"], ["W4c"], 640)
-        plus(T.pk[:], T.tt[:], T.uu[:], ["tt", "uu"], ["pk"])
+        for h in range(2):
+            lo, hi = 160 * h, 160 * h + 160
+            plus(T.pk[:, lo:hi], D[:, 2 * lo + 1:2 * hi:2], T.tt[:, lo:hi], ["tt%d" % h, "uu%d" % h], ["pk%d" % h])
     cpa(T.ob[:, 0:320], T.nat[:].indirect(SN), ["nat"] + snk, ["obs"])
     store("ops", T.op[:, 0:320], T.ob[0:128:16, 0:320], ["obs"])
-    ts(T.NR[:], T.ps5[:, 0:C], 0.0, C / UP, A.is_gt, A.mult, ["ps5"], ["NRa", "NRb"])
-    quant(T.xq3[:], T.xs3[:], T.xn2[:], ["xn2%d" % b for b in range(4)], ["xq3"])
-    mm(6, T.vq[:], T.vs[:], T.xq3[:], T.xs3[:], ["vq", "xq3"])
-    store("oc", T.oc[:, :], T.xq3[:, :].bitcast(dt.uint8), ["xq3"])
+    for h in range(2):
+        lo, hi = 160 * h, 160 * h + 160
+        quant(T.xq3[:, lo:hi], T.xs3[:, lo:hi], T.xn2[:, 4 * lo:4 * hi], ["xn2%d%d" % (b, h) for b in range(4)], ["xq3%d" % h])
+        mm(6 + h, T.vq[:], T.vs[:], T.xq3[:, lo:hi], T.xs3[:, lo:hi], ["vq", "xq3%d" % h], 160)
+        store("oc%d" % h, T.oc[:, 4 * lo:4 * hi], T.xq3[:, lo:hi].bitcast(dt.uint8), ["xq3%d" % h])
+        cpa(T.yb[:, lo:hi], T["ps%d" % (6 + h)][:, 0:160], ["ps%d" % (6 + h)], ["yb%d" % h])
+        if h == 0:
+            op("a", lambda: S.dma_start(T.y[:, lo:hi], T.yb[:, lo:hi]), ["yb0"], [], sem="sv_y0", inc=16)
+            ts(T.NR[:], T.ps5[:, 0:C], 0.0, C / UP, A.is_gt, A.mult, ["ps5"], ["NRa", "NRb"])
     for k in range(4):
-        store("os%d" % k, T.osc[4 * k:4 * k + 4, :], T.xs3[32 * k:32 * k + 4, :], ["xq3"])
-    cpa(T.yb[:], T.ps6[:, 0:C], ["ps6"], ["yb"])
-    store("y", T.y[:, :], T.yb[:], ["yb"])
+        store("os%d" % k, T.osc[4 * k:4 * k + 4, :], T.xs3[32 * k:32 * k + 4, :], ["xq30", "xq31"])
+    store("y1", T.y[:, 160:C], T.yb[:, 160:C], ["yb1"])
     pick(T.EN[:], T.NR[:], C, ["NRa", "NRb"], ["EN"])
     tt(T.rr[:, 0:20], T.EN[:, 15:C:16], T.bl[:, 40:60], A.add, ["EN", "bl2"], ["r0"])
     ts(T.lfa[:], T.rr[:, 0:20], CP, None, A.mult, None, ["r0", "cp"], ["lfa"])
-    ts(T.lfb[:], T.rr[:, 0:20], CP, float(C), A.mult, A.add, ["r0", "cp"], ["lfb"])
     w4 = ["W4a", "W4b", "W4c"]
-    scaled("v", T.ob[:, 320:640], T.W4[:, :].indirect(T.lfa[:]), 1, -1, w4 + ["lfa"], ["oba"])
-    scaled("a", T.ob[:, 640:960], T.W4[:, :].indirect(T.lfb[:]), 1, -1, w4 + ["lfb"], ["obb"])
+    scaled("v", T.ob[:, 320:640], T.W4[:, 0:3 * C].indirect(T.lfa[:]), 1, -1, w4 + ["lfa"], ["oba"])
+    scaled("a", T.ob[:, 640:960], T.W4[:, C:4 * C].indirect(T.lfa[:]), 1, -1, w4 + ["lfa"], ["obb"])
     store("opt", T.op[:, 320:960], T.ob[0:128:16, 320:960], ["oba", "obb"])
     learn("g", [(s, n) for s, n in count.items()])

from concourse.mybir import dt, AluOpType, ActivationFunctionType

STEP = [1, 2, 4]
C, STAGES = 320, 6
L = 1536
U = 2.0 ** -12
LOW = 1 - L * U
HT = 160
UP = 2.0 ** 24
MID = 480
WIN = L + 3 * C
NC = 20 + STAGES
CHAINS = [(0, 16), (16, 26)]
SHARE = [0, 0]
OWN = [0, 2, 2]
EARLY = [1, 4, 1]
FIRST = 12
HALF = 16 * (CHAINS[0][1] - STAGES)
BEFORE = [("v", 2, 0), ("a", 3, 0), ("v", 0, 1), ("a", 1, 1), ("a", 3, 1)]
AFTER = [("v", 2, 1)]
SCRATCH = {}


def _declare(names, where, cols, dtype):
    for n in names.split():
        SCRATCH[n] = (where, [128, cols], dtype)


F8, U8 = "float8_e4m3fn_x4", "uint8"
_declare("sti qq e16", "sbuf", 20, "int32")
_declare("tab tq", "sbuf", 60, "int32")
_declare("lci lq", "sbuf", NC, "int32")
_declare("kp kk", "sbuf", NC + 2, "int32")
_declare("d16 dd", "sbuf", 16, "int32")
_declare("lui", "sbuf", 8, "int32")
_declare("lu", "sbuf", 8, "uint16")
_declare("lk", "sbuf", NC + 2, "uint16")
_declare("ls lfa lfb pl0 pl1 pl2 pn", "sbuf", 20, "uint16")
_declare("lab", "sbuf", 40, "uint16")
_declare("lpos", "sbuf", 60, "uint16")
_declare("lc o0 o1 sc sn0 sn1 sn2", "sbuf", NC, "uint16")
_declare("rr pp bl ra", "sbuf", 64, "float32")
_declare("rt", "sbuf", 180, "float32")
_declare("sm", "sbuf", 8, "float32")
_declare("M", "sbuf", 16 * (NC + 2), "bfloat16")
_declare("G0 G1", "sbuf", 16 * NC, "float16")
_declare("E0 E1", "sbuf", 16 * (NC + len(CHAINS)), "float16")
_declare("NR EN X16", "sbuf", C, "float16")
_declare("b0 b0p", "sbuf", C, "float16")
_declare("D0 D1 D2", "sbuf", 2 * C, "float16")
_declare("G6 nat fin pk yb", "sbuf", C, "float32")
_declare("g1 sg x12 tt", "sbuf", C, "bfloat16")
_declare("W W6", "sbuf", WIN, "float32")
_declare("W4", "sbuf", 1280, "float32")
_declare("ob", "sbuf", 960, "float32")
_declare("one", "sbuf", 128, "bfloat16")
_declare("ui vi", "sbuf", 512, "bfloat16")
_declare("et", "sbuf", 516, "bfloat16")
_declare("xi ht z za xn0 xn1 xn2", "sbuf", 4 * C, "bfloat16")
_declare("t0 t1 t2 t3 w0 w1 w2 w3 h0 h1 h2 h3", "sbuf", C, "bfloat16")
for _q, _p, _n in (("wq", "wp", 512), ("uq", "us", 128), ("urq", "urs", 128), ("vq", "vs", 128), ("eq", "es", 512), ("hq", "hp", C), ("zq", "zp", C), ("iq", "ip", C)):
    _declare(_q, "sbuf", _n, F8)
    _declare(_p, "sbuf", _n, U8)
_declare("rq0 rq1 rq2 xq0 xq1 xq2 xq3", "sbuf", C, F8)
_declare("rp0 rp1 rp2 xs0 xs1 xs2 xs3", "sbuf", C, U8)
_declare("ps0 ps1 ps2 ps3 ps4 ps5 ps6 ps7", "psum", 512, "float32")
SEMAPHORES = ("cv ct ca cg sent gotl00 gotl01 gotl10 gotl11 gotl20 gotz0 gotz1 gotz2 ld_st ld_x ld_ta ld_tb ld_u ld_wc ld_ws ld_v "
              "sv_y0 sv_y1 sv_ops sv_opt sv_oc0 sv_oc1 sv_os0 sv_os1 sv_os2 sv_os3").split()


def rank_program(g, core, T, topo):
    rank = T.rank_of(core)
    if rank is None:
        return
    A, ACT = AluOpType, ActivationFunctionType
    queues = {"v": g.vector, "t": g.tensor, "a": g.scalar, "g": g, "y": g.sync}
    counter = {"v": "cv", "t": "ct", "a": "ca", "g": "cg"}
    count = {}
    known = {q: {} for q in queues}
    told = {}
    wrote, read = {}, {}

    def learn(q, tokens):
        need = {}
        for s, n in tokens:
            need[s] = max(need.get(s, 0), n)
        for s in sorted(need):
            n = need[s]
            if known[q].get(s, 0) >= n:
                continue
            queues[q].wait_ge(T.sem[s], n)
            known[q][s] = n
            for k, m in told.get((s, n), {}).items():
                known[q][k] = max(known[q].get(k, 0), m)

    def op(q, call, rd, wr, sem=None, inc=1):
        need = []
        for k in rd:
            need += wrote.get(k, [])
        for k in wr:
            need += wrote.get(k, []) + read.get(k, [])
        learn(q, need)
        s = sem or counter[q]
        call().then_inc(T.sem[s], inc)
        count[s] = count.get(s, 0) + inc
        tok = (s, count[s])
        told[tok] = dict(known[q])
        for k in rd:
            read.setdefault(k, []).append(tok)
        for k in wr:
            wrote[k], read[k] = [tok], []

    V, S, P = g.vector, g.scalar, g.tensor

    def keys(name, lo, hi):
        return ["%s:%d" % (name, i) for i in range(lo, hi)]

    def load(q, name, out, in_, key):
        op(q, lambda: queues[q].dma_start(out, in_), [], [key], sem="ld_" + name, inc=16)

    def store(name, out, in_, rd):
        op("y", lambda: g.sync.dma_start(out, in_), rd, [], sem="sv_" + name, inc=16)

    def iota(out, pattern, base, cm, wr, f32=False):
        if f32:
            op("g", lambda: g.iota(out, pattern, base, cm, allow_small_or_imprecise_dtypes=True), [], [wr])
        else:
            op("g", lambda: g.iota(out, pattern, base, cm), [], [wr])

    def cpg(out, in_, rd, wr, n=C):
        op("g", lambda: g.affine_select(out, in_, [[1, n]], A.is_ge, 0.0, 0, 0), rd, wr)

    def ts(out, in0, s1, s2, o0, o1, rd, wr):
        if o1 is None:
            op("v", lambda: V.tensor_scalar(out, in0, s1, None, o0), rd, wr)
        else:
            op("v", lambda: V.tensor_scalar(out, in0, s1, s2, o0, o1), rd, wr)

    def tt(out, a, b, o, rd, wr):
        op("v", lambda: V.tensor_tensor(out, a, b, o), rd, wr)

    def cpv(out, in_, rd, wr):
        op("v", lambda: V.tensor_copy(out, in_), rd, wr)

    def cpa(out, in_, rd, wr):
        op("a", lambda: S.activation(out, in_, ACT.Copy), rd, wr)

    def cp(q, out, in_, rd, wr):
        (cpv if q == "v" else cpa)(out, in_, rd, wr)

    def scaled(q, out, in_, scale, bias, rd, wr):
        if q == "a":
            op("a", lambda: S.activation(out, in_, ACT.Identity, bias=float(bias), scale=float(scale)), rd, wr)
        else:
            ts(out, in_, float(scale), float(bias), A.mult, A.add, rd, wr)

    def scan(out, d0, d1, init, o0, o1, rd, wr):
        op("v", lambda: V.tensor_tensor_scan(out, d0, d1, init, o0, o1), rd, wr)

    def pick(out, row, n, rd, wr, first=0):
        scan(out, T.M[:, first:first + n], row, 0.0, A.mult, A.add, rd + ["M"], wr)

    def plus(out, a, b, rd, wr):
        scan(out, a, b, 1.0, A.min, A.add, rd, wr)

    def quant(codes, plane, tile, rd, wr):
        op("v", lambda: V.quantize_mx(codes, plane, tile), rd, wr)

    def mm(bank, lq, lp, rq, rp, rd, n=C):
        op("t", lambda: P.matmul_mx(T["ps%d" % bank][:, 0:n], lq, lp, rq, rp, True, True), rd, ["ps%d" % bank])

    CP = T.sm[:, 0:1]
    CN = T.sm[:, 1:2]
    CQ = T.sm[:, 2:3]

    load("a", "u", T.ui[:], T.u[:], "ui")
    load("y", "x", T.xi[:], T.x[:], "xi")
    load("y", "st", T.sti[:], T.st[:], "sti")
    load("a", "ta", T.tab[:, 0:20], T.ta[:], "ta")
    load("y", "tb", T.tab[:, 20:40], T.tb[:], "tb")
    learn("y", wrote["xi"])
    load("y", "wc", T.wq[:, :].bitcast(dt.uint8), T.wc[:, :], "wq")
    load("y", "ws", T.wp[:, :], T.ws[:, :], "wp")
    load("y", "v", T.vi[:], T.v[:], "vi")

    def slot(w, k, lo=0, hi=C):
        first = k % 3 + L * (k // 3)
        return T[w][:, first + 3 * lo:first + 3 * hi - 2:3]

    IDN, POS = T.W[:, 3 * C:4 * C], T.W6[:, 3 * C:4 * C]
    op("v", lambda: V.memset(T.one[:], 1.0), [], ["one"])
    op("v", lambda: V.memset(T.et[:, :], 0.0), [], ["et"])
    iota(T.d16[:], [[1, 16]], 128, -1, "d16")
    iota(T.kp[:], [[0, NC + 2]], 0, 1, "kp")
    iota(T.lci[:], [[-1, NC]], NC - 1, 20, "lci")
    iota(T.lui[:], [[16, 8]], 0, 0, "lui")
    iota(T.W[:, 3 * C:L], [[1, L - 3 * C]], 1, 0, "idn", True)
    op("g", lambda: g.affine_select(T.et[:, 3:515:4], T.one[:], [[-1, 128]], A.is_equal, 0.0, 0, 1), ["one"], ["et"])
    iota(T.W6[:, 3 * C:L + 4], [[1, 29], [-16, 20]], 304 + 1, 0, "pos", True)
    iota(T.e16[:], [[16, 20]], 0, 0, "e16")
    ts(T.dd[:], T.d16[:], 15, None, A.bitwise_and, None, ["d16"], ["dd"])
    ts(T.kk[:], T.kp[:], 15, None, A.bitwise_and, None, ["kp"], ["kk"])
    ts(T.pp[:, 0:16], T.dd[:], 1, UP, A.is_equal, A.mult, ["dd"], ["p0"])
    ts(T.pp[:, 16:32], T.dd[:], 1, 1.0 / UP / L, A.is_ge, A.max, ["dd"], ["p1"])
    ts(T.lq[:], T.lci[:], -159.5, 1.0 / C, A.add, A.mult, ["lci"], ["lq"])
    cpv(T.lk[:], T.kk[:], ["kk"], ["lk"])
    tt(T.pp[:, 32:48], T.pp[:, 0:16], T.pp[:, 16:32], A.max, ["p0", "p1"], ["pm"])
    cpv(T.lu[:], T.lui[:], ["lui"], ["lu"])
    ts(T.rr[:, 0:NC], T.lq[:], -float(C), None, A.mult, None, ["lq"], ["r0"])
    ts(T.sm[:, 0:1], T.dd[:, 0:1], 1, UP, A.is_equal, A.mult, ["dd"], ["c0"])
    ts(T.sm[:, 1:2], T.dd[:, 0:1], 2, UP, A.is_equal, A.mult, ["dd"], ["c1"])
    ts(T.sm[:, 2:3], T.dd[:, 0:1], 1, 1.0 / UP, A.not_equal, A.max, ["dd"], ["cq"])
    tt(T.rr[:, 32:32 + NC], T.rr[:, 0:NC], T.lci[:], A.add, ["r0", "lci"], ["r1"])
    cpa(T.M[:, :], T.pp[:, 32:48].indirect(T.lk[:, :]), ["pm", "lk"], ["M"])
    ts(T.sm[:, 0:2], T.sm[:, 0:2], 1.0, None, A.max, None, ["c0", "c1"], ["cp"])
    cpv(T.ls[:], T.sti[:], ["sti"], ["ls"])
    cpv(T.lc[:], T.rr[:, 32:32 + NC], ["r1"], ["lc"])
    scaled("a", T.fin[:], IDN.indirect(T.ls[:]), 1 / UP, 0, ["idn", "ls"], ["fin"])
    quant(T.uq[:], T.us[:], T.ui[:], ["ui"], ["uq"])
    cpv(T.lab[:], T.tab[:, 0:40], ["ta", "tb"], ["lab"])
    cpv(T.urq[:, 0:128].bitcast(dt.uint32), T.uq[:, 0:128].bitcast(dt.uint32).indirect(T.lu[:, 0:8]), ["uq", "lu"], ["urq"])
    cpa(T.urs[:, 0:128], T.us[:, 0:128].indirect(T.lu[:, 0:8]), ["uq", "lu"], ["urs"])
    cpa(T.G1[:, :], T.fin[:].indirect(T.lc[:, :]), ["fin", "lc"], keys("G1", 0, NC))

    def scores(q, p):
        mm(4, T.urq[:], T.urs[:], T[q][:], T[p][:], ["urq", "urs", q])

    def signs(h):
        ts(T.tt[:, 160 * h:160 * h + 160], T["ps%d" % (6 + h)][:, 0:160], 0.0, LOW, A.is_gt, A.max, ["ps%d" % (6 + h)], ["tt%d" % h])

    def unpack(b, q, p):
        mm(b, T.eq[:, 128 * b:128 * b + 128], T.es[:, 128 * b:128 * b + 128], T[q][:], T[p][:], ["eq%d" % b, q, p])

    def own(b, r):
        cpa(T["t%d" % b][:], T["ps%d" % b][:, 0:C], ["ps%d" % b], ["t%d" % b])
        unpack(b, "rq%d" % r, "rp%d" % r)

    def unit(b):
        quant(T.eq[:, 128 * b:128 * b + 128], T.es[:, 128 * b:128 * b + 128], T.et[:, 3 - b:515 - b], ["et"], ["eq%d" % b])
        unpack(b, "xq0", "xs0")

    def partner(r):
        other = T.cores[rank ^ STEP[r]]
        return topo.addr(other)[0:2] + (topo.mask(core, other), len(topo.engines(core, other)))

    def send_state(r):
        rid, pid, mask, ne = partner(r)
        xq, xs, rq, rp, sem = [n + str(r) for n in ("xq", "xs", "rq", "rp", "gotz")]
        learn("g", wrote[xq] + wrote.get(xs, []))
        g.remote_dma(T[rq][:, :].bitcast(dt.uint8), T[xq][:, :].bitcast(dt.uint8), T.sem[sem], T.sem.sent, pid, rid, mask)
        g.remote_dma(T[rp][:, :], T[xs][:, :], T.sem[sem], T.sem.sent, pid, rid, mask)
        count["sent"] = count.get("sent", 0) + 2 * ne
        wrote[rq] = [(sem, 2 * ne)]

    scaled("v", T.b0[:], IDN, 3 * U, -2 * U, ["idn"], ["b0"])
    quant(T.iq[:], T.ip[:], T.xi[:], ["xi"], ["iq"])
    scores("iq", "ip")
    cpv(T.xq0[:, :].bitcast(dt.uint32), T.iq[:, :].bitcast(dt.uint32).indirect(T.lc[:, STAGES:NC]), ["iq", "lc"], ["xq0"])
    cpa(T.xs0[:, :], T.ip[:, :].indirect(T.lc[:, STAGES:NC]), ["iq", "lc"], ["xs0"])
    send_state(0)
    ts(T.tt[:], T.ps4[:, 0:C], 0.0, LOW, A.is_gt, A.max, ["ps4"], ["tt0", "tt1"])
    pick(T.E1[:, 0:16 * NC], T.G1[:, :], 16 * NC, keys("G1", 0, NC), keys("E1", 0, NC))
    plus(T.pk[:], T.b0[:], T.tt[:], ["tt0", "tt1", "b0"], ["pk0", "pk1"])
    ts(T.sc[:, :], T.E1[:, 15:16 * NC:16], CP, -1.0, A.mult, A.add, keys("E1", 0, NC) + ["cp"], keys("sc", 0, NC))
    scaled("a", slot("W6", 0), POS.indirect(T.lab[:, 0:20]), 1 / UP, 0, ["pos", "lab"], ["W60"])
    W6K = ["W60", "W61a", "W61b", "W62", "pos", "W63", "W64", "W65"]
    WK = ["W0", "W1", "W2", "W3", "W4", "W5", "idn"]

    for r in range(3):
        rid, pid, mask, ne = partner(r)
        rq, rp, sn, pl, xn = [n + str(r) for n in ("rq", "rp", "sn", "pl", "xn")]
        lab, sc = ("lab", "sc") if r == 0 else ("lpos", "sn%d" % (r - 1))
        small = (1 / U / UP, -(LOW / U + 1 + MID) / UP)
        last = r == 2

        def gather(n, lo, hi, q):
            G, o = "G%d" % (n % 2), "o%d" % ((n + 1) % 2)
            if n == 0:
                scaled(q, T.G0[:, 16 * lo:16 * hi], T.pk[:].indirect(T[sc][:, lo:hi]), small[0], small[1], ["pk0", "pk1"] + keys(sc, lo, hi), keys(G, lo, hi))
            elif n == STAGES and last:
                cp(q, T.G6[:, 16 * (lo - n):16 * (hi - n)], T.W6[:, 0:WIN].indirect(T[o][:, lo:hi]), W6K + keys(o, lo, hi), keys("G6", lo, hi))
            else:
                win, wk = (T.W, WK) if n < STAGES else (T.W6, W6K)
                cp(q, T[G][:, 16 * lo:16 * hi], win[:, 0:WIN].indirect(T[o][:, lo:hi]), wk + keys(o, lo, hi), keys(G, lo, hi))

        def row(n, lo, hi, i):
            G, E = "G%d" % (n % 2), "E%d" % (n % 2)
            pick(T[E][:, 16 * (lo + i):16 * (hi + i)], T[G][:, 16 * lo:16 * hi], 16 * (hi - lo), keys(G, lo, hi), keys(E, lo + i, hi + i))

        def cast(n, lo, hi, i):
            E = "E%d" % (n % 2)
            o, more = ("o%d" % (n % 2), MID) if n < STAGES else (sn, -1)
            ts(T[o][:, lo:hi], T[E][:, 16 * (lo + i) + 15:16 * (hi + i):16], CP, float(more), A.mult, A.add, keys(E, lo + i, hi + i) + ["cp"], keys(o, lo, hi))

        scaled("a", slot("W", 0), T.pk[:].indirect(T[lab][:, 0:20]), small[0], small[1], ["pk0", "pk1", lab], ["W0"])
        scaled("v", slot("W", 1), T.pk[:].indirect(T[lab][:, 20:40]), small[0], small[1], ["pk0", "pk1", lab], ["W1"])
        gather(0, 0, FIRST, "v")
        gather(0, FIRST, NC, "a")
        cpg(slot("W", 3), slot("W", 0), ["W0"], ["W3"])
        cpa(slot("W", 2), slot("W", 0), ["W0"], ["W2"])
        cpv(slot("W", 4), slot("W", 1), ["W1"], ["W4"])
        cpa(slot("W", 5), slot("W", 0), ["W0"], ["W5"])
        row(0, 0, NC, 0)
        if r == 0:
            unit(0)
        cast(0, 0, NC, 0)
        gaps, fill = [], []
        if r == 0:
            for k in (2, 3, 5):
                cpg(slot("W6", k), slot("W6", 0), ["W60", "pos"], ["W6%d" % k])
            scaled("a", slot("W6", 1, 0, 160), POS.indirect(T.lab[:, 20:30]), 1 / UP, 0, ["pos", "lab"], ["W61a"])

            def rest():
                scaled("a", slot("W6", 1, 160, C), POS.indirect(T.lab[:, 30:40]), 1 / UP, 0, ["pos", "lab"], ["W61b"])
                cpg(slot("W6", 4), slot("W6", 1), ["W61a", "W61b", "pos"], ["W64"])
                iota(T.nat[:], [[-1, 20], [20, 16]], 19, 0, "nat", True)
            gaps.append(rest)
            tab = ["ta", "tb", "tc"]
            fill += [(lambda b=b: unit(b)) for b in range(1, 4)]
            fill += [lambda: tt(T.tab[:, 40:60], T.e16[:], T.kk[:, 0:20], A.add, ["e16", "kk"], ["tc"]),
                     lambda: ts(T.tq[:], T.tab[:], -9.5, 0.05, A.add, A.mult, tab, ["tq"]),
                     lambda: ts(T.rt[:, 0:60], T.tab[:], -16.0, 304.0, A.mult, A.add, tab, ["rt0"]),
                     lambda: ts(T.rt[:, 60:120], T.tq[:], 321.0, None, A.mult, None, ["tq"], ["rt1"]),
                     lambda: tt(T.rt[:, 120:180], T.rt[:, 0:60], T.rt[:, 60:120], A.add, ["rt0", "rt1"], ["rt2"]),
                     lambda: cpv(T.lpos[:], T.rt[:, 120:180], ["rt2"], ["lpos"])]
        if r == 1:
            fill += [lambda: op("v", lambda: V.memset(T.D0[:, 0:2 * C:2], 0.0), [], ["D0e"]),
                     lambda: ts(T.D0[:, 1:2 * C:2], T.g1[:], -2.0, U, A.mult, A.add, ["g0", "g1"], ["D0o"]),
                     lambda: quant(T.vq[:], T.vs[:], T.vi[:], ["vi"], ["vq"]),
                     lambda: ts(T.bl[:, 0:20], T.tab[:, 40:60], CQ, None, A.mult, None, ["tc", "cq"], ["bl0"])]
        if last:
            fill += [lambda: scan(T.x12[:], T.D2[:, 1:2 * C:2], T.b0p[:], 0.0, A.max, A.subtract, ["uu0", "uu1", "b0p"], ["x12"])]
            fill += [None] * 5
            fill += [lambda: pick(T.EN[:], T.X16[:], C, ["X16"], ["EN"]),
                     lambda: ts(T.bl[:, 20:40], T.EN[:, 15:C:16], CP, 0.5, A.mult, A.is_gt, ["EN", "cp"], ["bl1"]),
                     lambda: ts(T.bl[:, 20:40], T.bl[:, 20:40], CQ, float(C), A.mult, A.mult, ["bl1", "cq"], ["bl1"]),
                     lambda: tt(T.bl[:, 40:60], T.bl[:, 20:40], T.bl[:, 0:20], A.add, ["bl0", "bl1"], ["bl2"])]

        gaps += [(lambda b=b: own(b, r)) for b in range(OWN[r], 4)]
        if last:
            gaps[1:1] = [lambda h=h: scaled("a", T.X16[:, 160 * h:160 * h + 160], T.x12[:].indirect(T.lpos[:, 40 + 10 * h:50 + 10 * h]),
                                            1 / U / UP, 0, ["x12", "lpos"], ["X16"]) for h in range(2)]
        gaps += [(lambda b=b: cpa(T["w%d" % b][:], T["ps%d" % b][:, 0:C], ["ps%d" % b], ["w%d" % b])) for b in range(EARLY[r])]
        steps = [(n, i) for n in range(1, STAGES + 1) for i in range(2)]
        parts = ((0, HALF), (HALF, C))

        def send_list(lo, hi, i):
            learn("g", [tok for k in keys(sn, lo, hi) for tok in wrote[k]])
            g.remote_dma(T[pl][:, lo - STAGES:hi - STAGES], T[sn][:, lo:hi], T.sem["gotl%d%d" % (r, i)], T.sem.sent, pid, rid, mask)
            count["sent"] += ne
            wrote[pl + str(i)] = [("gotl%d%d" % (r, i), ne)]

        def mosaic(q, b, h):
            lo, hi = parts[h]
            a, e = STAGES + lo // 16, STAGES + hi // 16
            cp(q, T.z[:, 4 * lo + b:4 * hi:4], T["t%d" % b][:].indirect(T[sn][:, a:e]), ["t%d" % b] + keys(sn, a, e), ["z%d%d" % (b, h)])

        def span(n, i):
            return (max(CHAINS[i][0], n - n % 2), CHAINS[i][1])

        for t in range(len(steps) + 1):
            n, i = steps[t - 1]
            behind = t > 0 and not (last and n == STAGES)
            if behind:
                row(n, span(n, i)[0] - (i if n < STAGES else 0), span(n, i)[1], i)
            if t == len(steps) and not last:
                mosaic("v", 0, 0)
                mosaic("a", 1, 0)
            if t < len(steps):
                lo, hi = span(*steps[t])
                cut = (lo + hi) // 4 * 2 + SHARE[steps[t][1]]
                gather(steps[t][0], lo, cut, "v")
                gather(steps[t][0], cut, hi, "a")
                if steps[t][1] == 1 and gaps:
                    gaps.pop(0)()
            if behind:
                cast(n, span(min(n + 1, STAGES), i)[0], span(n, i)[1], i)
                if n == STAGES:
                    send_list(span(n, i)[0], span(n, i)[1], i)
            if (t > 1 or r == 0) and fill:
                (fill.pop(0) or list)()
            if t == len(steps) and not last:
                break
        if last:
            cpv(T.NR[:, 0:160], T.G6[:, :].indirect(T.lpos[:, 40:50]), keys("G6", STAGES, NC) + ["lpos"], ["NRa"])
            cpa(T.NR[:, 160:320], T.G6[:, :].indirect(T.lpos[:, 50:60]), keys("G6", STAGES, NC) + ["lpos"], ["NRb"])
            pick(T.EN[:], T.NR[:], C, ["NRa", "NRb"], ["EN"])
            ts(T[sn][:, STAGES:NC], T.EN[:, 15:C:16], CP, -1.0, A.mult, A.add, ["EN", "cp"], keys(sn, STAGES, NC))
        snk, SN = keys(sn, STAGES, NC), T[sn][:, STAGES:NC]
        if last:
            send_list(STAGES, NC, 0)
            wrote[pl + "1"] = wrote[pl + "0"]
            mosaic("v", 0, 0)
            mosaic("a", 1, 0)
        for k in range(EARLY[r], 4):
            cp("av"[k % 2], T["w%d" % k][:], T["ps%d" % k][:, 0:C], ["ps%d" % k], ["w%d" % k])
        for q, b, h in BEFORE:
            mosaic(q, b, h)

        def lay(b, h):
            lo, hi = parts[h]
            cp("av"[b // 2], T.za[:, 4 * lo + b:4 * hi:4], T["w%d" % b][:].indirect(T[pl][:, lo // 16:hi // 16]), ["w%d" % b, pl + str(h)], ["za%d%d" % (b, h)])

        def answer(h):
            lo, hi = parts[h]
            quant(T.zq[:, lo:hi], T.zp[:, lo:hi], T.za[:, 4 * lo:4 * hi], ["za%d%d" % (b, h) for b in range(4)], ["zq%d" % h])
            for b in range(4 if h else 2):
                lo, hi = parts[h] if b < 2 else (0, C)
                mm(b + (4 * h if b < 2 else 0), T.wq[:, 128 * b:128 * b + 128], T.wp[:, 128 * b:128 * b + 128], T.zq[:, lo:hi], T.zp[:, lo:hi],
                   ["wq", "wp", "zq0", "zq%d" % h], hi - lo)

        def scale(q, b, h):
            lo, hi = parts[h] if b < 2 else (0, C)
            bank = "ps%d" % (4 * h + b)
            scaled(q, T["h%d" % b][:, lo:hi], T[bank][:, 0:hi - lo], 0.03125, 0, [bank], ["h%d%d" % (b, h)])

        for b in (0, 2, 1, 3):
            lay(b, 0)
        if last:
            ts(T.qq[:], T[pl][:], -7.5, 1.0 / 16, A.add, A.mult, [pl + "0"], ["qq"])
        lay(0, 1)
        lay(2, 1)
        answer(0)
        lay(1, 1)
        lay(3, 1)
        if last:
            ts(T.ra[:, 0:20], T[pl][:], 20.0, 19.0, A.mult, A.add, [pl + "0"], ["ra0"])
            ts(T.ra[:, 20:40], T.qq[:], -321.0, None, A.mult, None, ["qq"], ["ra1"])
        answer(1)
        hl = "pn" if last else pl
        if not last:
            pick(T.EN[:, 0:96], T.G0[:, 16 * 20:16 * NC], 96, keys("G0", 20, NC), ["EN"], 15)
            mosaic(*AFTER[0])
            ts(T[sn][:, 0:STAGES], T.EN[:, 15:96:16], CN, -1.0, A.mult, A.add, ["EN", "cp"], keys(sn, 0, STAGES))
        else:
            tt(T.ra[:, 40:60], T.ra[:, 0:20], T.ra[:, 20:40], A.add, ["ra0", "ra1"], ["ra2"])
            mosaic(*AFTER[0])
            cpv(T.pn[:], T.ra[:, 40:60], ["ra2"], ["pn"])
        for q, b, h in AFTER[1:]:
            mosaic(q, b, h)
        scale("a", 0, 0)
        scale("a", 1, 0)
        scale("a", 0, 1)
        scale("a", 1, 1)
        xq, xs = "xq%d" % (r + 1), "xs%d" % (r + 1)
        for b in range(4):
            if b >= 2:
                scale("a", b, 0)
            if b == 0:
                cpg(T.ht[:, 0:4 * C:4], T.h0[:], ["h00", "h01"], ["ht0"])
                cpg(T.ht[:, 1:4 * HT:4], T.h1[:, 0:HT], ["h10", "h11"], ["ht4"], HT)
            if b == 3:
                cpa(T.ht[:, 4 * HT + 1:4 * C:4], T.h1[:, HT:C], ["h10", "h11"], ["ht1"])
                for k in range(2, 4):
                    cpa(T.ht[:, k:4 * C:4], T["h%d" % k][:], ["h%d0" % k], ["ht%d" % k])
                quant(T.hq[:], T.hp[:], T.ht[:], ["ht%d" % k for k in range(5)], ["hq"])
                mm(5, T.urq[:], T.urs[:], T.hq[:], T.hp[:], ["urq", "urs", "hq"])
                if r == 0:
                    scaled("a", T.b0p[:], T.nat[:], 3 * U, U, ["nat"], ["b0p"])
                    cpa(T.W4[:, 0:320], IDN.indirect(T.lab[:, 0:20]), ["idn", "lab"], ["W4a"])
                if r == 1:
                    cpa(T.W4[:, 320:640], IDN.indirect(T.lab[:, 20:40]), ["idn", "lab"], ["W4b"])
            for lo, hi, hs in ([(0, C, "01")] if b < 3 else [(0, 160, "0"), (160, C, "1")]):
                tt(T[xn][:, 4 * lo + b:4 * hi:4], T["h%d" % b][:].indirect(T[hl][:, lo // 16:hi // 16]), T.z[:, 4 * lo + b:4 * hi:4], A.add,
                   ["h%d0" % b, "h%d1" % b, hl, pl + "0", pl + "1", "z%d0" % b, "z%d1" % b], [xn + str(b) + h for h in hs])
        if last:
            break
        for h in range(2):
            lo, hi = 160 * h, 160 * h + 160
            quant(T[xq][:, lo:hi], T[xs][:, lo:hi], T[xn][:, 4 * lo:4 * hi], [xn + str(b) + str(h) for b in range(4)], [xq + "h%d" % h])
            mm(6 + h, T.urq[:], T.urs[:], T[xq][:, lo:hi], T[xs][:, lo:hi], ["urq", "urs", xq + "h%d" % h], 160)
        wrote[xq] = wrote[xq + "h1"]
        send_state(r + 1)
        for b in range(4):
            unpack(b, xq, xs)
        D = T.D1 if r == 0 else T.D2
        for h in range(2):
            lo, hi = 160 * h, 160 * h + 160
            op("a", lambda: S.activation(T.sg[:, lo:hi], T.ps5[:, lo:hi], ACT.Sign), ["ps5"], ["sg%d" % h])
        for h in range(2):
            lo, hi = 160 * h, 160 * h + 160
            out, scl = (T.g1[:, lo:hi], U) if r == 0 else (T.D1[:, 2 * lo:2 * hi:2], 1.0)
            op("a", lambda: S.activation(out, T.sg[:, lo:hi], ACT.Relu, scale=scl), ["sg%d" % h], ["g%d" % h if r == 0 else "D1e%d" % h])
        for h in range(2):
            lo, hi = 160 * h, 160 * h + 160
            signs(h)
            if r == 0:
                plus(T.D1[:, 2 * lo + 1:2 * hi:2], T.g1[:, lo:hi], T.b0p[:, lo:hi], ["g%d" % h, "b0p"], ["uu%d" % h])
            else:
                scan(T.D2[:, 2 * lo:2 * hi], T.D0[:, 2 * lo:2 * hi], T.D1[:, 2 * lo:2 * hi], 0.0, A.mult, A.add, ["D0e", "D0o", "D1e%d" % h], ["uu%d" % h])
        for b in range(OWN[r + 1]):
            own(b, r + 1)
        if r == 1:
            cpg(T.W4[:, 640:1280], T.W4[:, 0:640], ["W4a", "W4b"], ["W4c"], 640)
        for h in range(2):
            lo, hi = 160 * h, 160 * h + 160
            plus(T.pk[:, lo:hi], D[:, 2 * lo + 1:2 * hi:2], T.tt[:, lo:hi], ["tt%d" % h, "uu%d" % h], ["pk%d" % h])
    cpa(T.ob[:, 0:320], T.nat[:].indirect(SN), ["nat"] + snk, ["obs"])
    store("ops", T.op[:, 0:320], T.ob[0:128:16, 0:320], ["obs"])
    for h in range(2):
        lo, hi = 160 * h, 160 * h + 160
        quant(T.xq3[:, lo:hi], T.xs3[:, lo:hi], T.xn2[:, 4 * lo:4 * hi], ["xn2%d%d" % (b, h) for b in range(4)], ["xq3%d" % h])
        mm(6 + h, T.vq[:], T.vs[:], T.xq3[:, lo:hi], T.xs3[:, lo:hi], ["vq", "xq3%d" % h], 160)
        store("oc%d" % h, T.oc[:, 4 * lo:4 * hi], T.xq3[:, lo:hi].bitcast(dt.uint8), ["xq3%d" % h])
        cpa(T.yb[:, lo:hi], T["ps%d" % (6 + h)][:, 0:160], ["ps%d" % (6 + h)], ["yb%d" % h])
        if h == 0:
            op("a", lambda: S.dma_start(T.y[:, lo:hi], T.yb[:, lo:hi]), ["yb0"], [], sem="sv_y0", inc=16)
            ts(T.NR[:], T.ps5[:, 0:C], 0.0, C / UP, A.is_gt, A.mult, ["ps5"], ["NRa", "NRb"])
    for k in range(4):
        store("os%d" % k, T.osc[4 * k:4 * k + 4, :], T.xs3[32 * k:32 * k + 4, :], ["xq30", "xq31"])
    store("y1", T.y[:, 160:C], T.yb[:, 160:C], ["yb1"])
    pick(T.EN[:], T.NR[:], C, ["NRa", "NRb"], ["EN"])
    tt(T.rr[:, 0:20], T.EN[:, 15:C:16], T.bl[:, 40:60], A.add, ["EN", "bl2"], ["r0"])
    ts(T.lfa[:], T.rr[:, 0:20], CP, None, A.mult, None, ["r0", "cp"], ["lfa"])
    w4 = ["W4a", "W4b", "W4c"]
    scaled("v", T.ob[:, 320:640], T.W4[:, 0:3 * C].indirect(T.lfa[:]), 1, -1, w4 + ["lfa"], ["oba"])
    scaled("a", T.ob[:, 640:960], T.W4[:, C:4 * C].indirect(T.lfa[:]), 1, -1, w4 + ["lfa"], ["obb"])
    store("opt", T.op[:, 320:960], T.ob[0:128:16, 320:960], ["oba", "obb"])
    learn("g", [(s, n) for s, n in count.items()])
